import numpy as np
import ml_dtypes


def mxq(x, axis, fmt="e4m3"):
    dtype, down = {"e4m3": (ml_dtypes.float8_e4m3fn, 7), "e5m2": (ml_dtypes.float8_e5m2, 14)}[fmt]
    v = np.moveaxis(np.asarray(x, np.float32).astype(ml_dtypes.bfloat16).astype(np.float64), axis, -1)
    blocks = v.reshape(v.shape[:-1] + (-1, 32))
    amax = np.abs(blocks).max(-1, keepdims=True)
    byte = np.maximum(np.where(amax > 0, np.frexp(amax)[1] - 1 + 127, 0) - down, 1)
    scale = np.exp2(byte - 127.0)
    codes = (blocks / scale).astype(np.float32).astype(dtype).astype(np.float64)
    return np.moveaxis((codes * scale).reshape(v.shape), -1, axis)


WIDE = False


def mx_kscale(k):
    if not WIDE:
        return np.ones(k)
    levels = np.array([10, -10, 5, -5, 0])
    if k % 512:
        return np.exp2(np.random.permutation(np.resize(levels, k // 32))).repeat(32)
    a = np.empty((k // 512, 16))
    for p in range(k // 512):
        a[p, :8] = np.random.permutation(np.resize(levels, 8))
        for g in range(8):
            far = levels[np.abs(levels - a[p, g]) >= 10]
            a[p, g + 8] = far[np.random.randint(len(far))]
    return np.exp2(a.ravel()).repeat(32)


def f64(x):
    return np.asarray(x).astype(np.float64)


def striped(idx):
    return np.tile(idx.reshape(-1, 16).T, (8, 1)).astype(np.uint16)


def unstriped(offs):
    return offs[:16].T.reshape(-1).astype(np.int64)


E2M1 = np.array([0.0, 0.5, 1.0, 1.5, 2.0, 3.0, 4.0, 6.0, -0.0, -0.5, -1.0, -1.5, -2.0, -3.0, -4.0, -6.0])


def pack_weight(w, fmt):
    k, n = w.shape
    w = f64(np.asarray(w, np.float32).astype(ml_dtypes.bfloat16)).reshape(k // 32, 32, n)
    amax = np.abs(w).max(1)
    if fmt == "e4m3":
        byte = np.frexp(amax)[1] - 1 + 127 - 7
    else:
        mant, ex = np.frexp(amax / 6.0)
        byte = np.where(mant > 0.5, ex, ex - 1) + 127
    byte = np.clip(np.where(amax > 0, byte, 1), 1, 254)
    scaled = (w * np.exp2(127.0 - byte)[:, None, :]).reshape(k, n).astype(np.float32)
    by_word = np.ascontiguousarray(scaled.reshape(k // 512, 128, 4, n).transpose(0, 1, 3, 2))
    if fmt == "e4m3":
        words = by_word.astype(ml_dtypes.float8_e4m3fn).view(np.uint8)
    else:
        c = by_word.astype(ml_dtypes.float4_e2m1fn).view(np.uint8) & 0xF
        words = (c[..., 0::2] | (c[..., 1::2] << 4)).reshape(k // 512, 128, 2 * n)
    return np.ascontiguousarray(words), np.ascontiguousarray(byte.astype(np.uint8).reshape(k // 512, 16, n))


def unpack_weight(words, scales, fmt):
    g, _, n = scales.shape
    words = np.ascontiguousarray(words).reshape(g, 128, n, -1)
    if fmt == "e4m3":
        vals = words.view(ml_dtypes.float8_e4m3fn).astype(np.float64)
    else:
        nib = np.empty((g, 128, n, 4), np.uint8)
        nib[..., 0::2] = words & 0xF
        nib[..., 1::2] = words >> 4
        vals = E2M1[nib]
    vals = vals * np.repeat(np.exp2(scales.astype(np.float64) - 127.0), 8, axis=1)[..., None]
    return vals.transpose(0, 1, 3, 2).reshape(g * 512, n)


def gelu(v):
    return 0.5 * v * (1.0 + np.tanh(np.sqrt(2.0 / np.pi) * (v + 0.044715 * v**3)))


K, H, N, T, S = 1536, 1024, 512, 2048, 1024


def setup_inputs():
    n = np.random.standard_normal
    s = mx_kscale(K)[:, None]
    u = mx_kscale(H)[:, None]
    tab_words, tab_scales = pack_weight(n((K, T)) * s, "e4m3")
    offs = striped(np.random.permutation(T)[:S])
    w1 = (n((K, H)) / np.sqrt(K) / s * u.T).astype(np.float32)
    b1 = (0.5 * n(H) * u[:, 0]).astype(np.float32)
    w4_words, w4_scales = pack_weight(1.2 * n((H, N)) / np.sqrt(H) / u, "e2m1")
    gT = n((N, T)).astype(np.float32)
    wgt = np.exp(0.3 * n(N)).astype(np.float32)
    return {"tab_words": tab_words, "tab_scales": tab_scales, "offs": offs,
            "w1": w1, "b1": b1, "w4_words": w4_words, "w4_scales": w4_scales,
            "gT": gT, "wgt": wgt}


def reference(tab_words, tab_scales, offs, w1, b1, w4_words, w4_scales, gT, wgt):
    v = unpack_weight(tab_words, tab_scales, "e4m3")[:, unstriped(offs)]
    w1q = mxq(f64(w1), 0, "e4m3")
    w4 = unpack_weight(w4_words, w4_scales, "e2m1")
    g = f64(gT)[:, unstriped(offs)]
    h = np.maximum((w1q.T @ v) + f64(b1)[:, None], 0.0)
    hq = mxq(h, 0, "e4m3")
    y = w4.T @ hq
    return np.abs(y - g) * f64(wgt)[:, None]

@@ -1,0 +1,224 @@
+from contextlib import ExitStack
+
+import concourse.mybir as mybir
+
+K, H, N, T, S = 1536, 1024, 512, 2048, 1024
+FLOPS = 2 * S * (K * H + H * N)
+
+F32 = mybir.dt.float32
+BF16 = mybir.dt.bfloat16
+I32 = mybir.dt.int32
+U32 = mybir.dt.uint32
+U16 = mybir.dt.uint16
+U8 = mybir.dt.uint8
+FP8X4 = mybir.dt.float8_e4m3fn_x4
+FP4X4 = mybir.dt.float4_e2m1fn_x4
+ACT = mybir.ActivationFunctionType
+ALU = mybir.AluOpType
+
+P = 128
+PACK = 4
+KP = P * PACK
+KA = K // KP
+HB = H // KP
+NC = N // P
+TOK = 512
+SH = S // TOK
+OC = TOK // 16
+
+
+def tile_list_flow_anomaly_residuals_kernel(tc, tab_words, tab_scales, offs, w1, b1, w4_words, w4_scales, gT, wgt, out):
+    nc = tc.nc
+    with ExitStack() as ctx:
+        lists = ctx.enter_context(tc.tile_pool(name="lists", bufs=1))
+        keep = ctx.enter_context(tc.tile_pool(name="keep", bufs=1))
+        psum = ctx.enter_context(tc.psum_pool(name="psum", bufs=1))
+
+        offsets = lists.tile([P, S // 16], U16, name="offsets")
+        words = [keep.tile([P, T], I32, name=f"words{a}", align_bytes=64) for a in range(KA)]
+        tscale = keep.tile([P, T // 4], I32, name="tscale", align_bytes=64)
+        vcodes = [[keep.tile([P, TOK], I32, name=f"vcodes{a}_{s}", align_bytes=64) for s in range(SH)] for a in range(KA)]
+        vscale = [keep.tile([P, TOK], U8, name=f"vscale{s}", align_bytes=64) for s in range(SH)]
+        raw = [[keep.tile([P, PACK, KP], F32, name=f"raw{b}_{a}", align_bytes=64) for a in range(KA)] for b in range(HB)]
+        wbf3 = [keep.tile([P, PACK * KP], BF16, name=f"wbf{a}", align_bytes=64) for a in range(KA)]
+        wbf = [wbf3 for b in range(HB)]
+        wcodes = [[keep.tile([P, KP], U32, name=f"wcodes{b}_{a}", align_bytes=64) for a in range(KA)] for b in range(HB)]
+        wscale = [[keep.tile([P, KP], U8, name=f"wscale{b}_{a}", align_bytes=64) for a in range(KA)] for b in range(HB)]
+        bias = keep.tile([P, HB, PACK], F32, name="bias")
+        weight = keep.tile([P, NC], F32, name="weight")
+        w4c = keep.tile([P, HB, 2 * N], U8, name="w4c", align_bytes=64)
+        w4s = keep.tile([P, HB, N // 4], I32, name="w4s", align_bytes=64)
+        gwin = [keep.tile([P, T], F32, name=f"gwin{c}", align_bytes=64) for c in range(NC)]
+        gpick = [[keep.tile([P, TOK], F32, name=f"gpick{c}_{s}", align_bytes=64) for s in range(SH)] for c in range(NC)]
+        hrow = [[keep.tile([P, PACK, TOK], BF16, name=f"hrow{b}_{s}", align_bytes=64) for s in range(SH)] for b in range(HB)]
+        hint2 = [keep.tile([P, PACK * TOK], BF16, name=f"hint{s}", align_bytes=64) for s in range(SH)]
+        hint = [hint2 for b in range(HB)]
+        hcodes = [[keep.tile([P, TOK], U32, name=f"hcodes{b}_{s}", align_bytes=64) for s in range(SH)] for b in range(HB)]
+        hscale = [[keep.tile([P, TOK], U8, name=f"hscale{b}_{s}", align_bytes=64) for s in range(SH)] for b in range(HB)]
+        diff = [[keep.tile([P, TOK], F32, name=f"diff{c}_{s}", align_bytes=64) for s in range(SH)] for c in range(NC)]
+        banks = [[psum.tile([P, TOK], F32, name=f"bank{s}_{t}") for t in range(PACK)] for s in range(SH)]
+
+        def offs_of(s):
+            return offsets[:, s * OC : (s + 1) * OC]
+
+        def load_w1(b, a):
+            src = w1[a * KP : (a + 1) * KP, b * KP : (b + 1) * KP]
+            nc.sync.dma_start(out=raw[b][a][:], in_=src.rearrange("(p j) c -> p j c", j=PACK))
+
+        def load_words(a):
+            nc.sync.dma_start(out=words[a][:], in_=tab_words[a].rearrange("p t i -> p (t i)").bitcast(I32))
+
+        def cast_w1(b, a, m0, m1, eng):
+            dst = wbf[b][a][:].rearrange("p (t m j) -> p m j t", t=PACK, j=PACK)[:, m0:m1]
+            src = raw[b][a][:].rearrange("p j (m t) -> p m j t", t=PACK)[:, m0:m1]
+            if eng == "V":
+                nc.vector.tensor_copy(out=dst, in_=src)
+            else:
+                nc.scalar.copy(out=dst, in_=src)
+
+        def quant_w1(b, a):
+            nc.vector.quantize_mx(out=wcodes[b][a][:].bitcast(FP8X4), scales=wscale[b][a][:], in_=wbf[b][a][:])
+
+        def gather_words(a, s):
+            nc.vector.tensor_copy(vcodes[a][s][:].bitcast(U32), words[a][:].bitcast(U32).indirect(offs_of(s)))
+
+        def gather_scales(s):
+            nc.vector.tensor_copy(vscale[s][:], tscale[:].bitcast(U8).indirect(offs_of(s)))
+
+        def mm1(b, a, s):
+            for t in range(PACK):
+                cols = slice(t * P, (t + 1) * P)
+                nc.tensor.matmul_mx(
+                    out=banks[s][t][:],
+                    lhsT=wcodes[b][a][:, cols].bitcast(FP8X4),
+                    lhsT_scale=wscale[b][a][:, cols],
+                    rhs=vcodes[a][s][:].bitcast(FP8X4),
+                    rhs_scale=vscale[s][PACK * a : P, :],
+                    start=(a == 0),
+                    stop=(a == KA - 1),
+                )
+
+        def evac_h(b, s):
+            for t in range(PACK):
+                nc.scalar.activation(out=hrow[b][s][:, t, :], in_=banks[s][t][:], func=ACT.Relu, bias=bias[:, b, t : t + 1])
+
+        def weave_h(b, s, c0, c1, eng):
+            dst = hint[b][s][:].rearrange("p (c i t) -> p c t i", i=4, t=PACK)[:, c0:c1]
+            src = hrow[b][s][:].rearrange("p t (c i) -> p c t i", i=4)[:, c0:c1]
+            if eng == "V":
+                nc.vector.tensor_copy(out=dst, in_=src)
+            else:
+                nc.scalar.copy(out=dst, in_=src)
+
+        def quant_h(b, s):
+            nc.vector.quantize_mx(out=hcodes[b][s][:].bitcast(FP8X4), scales=hscale[b][s][:], in_=hint[b][s][:])
+
+        def mm2(b, s):
+            for c in range(NC):
+                nc.tensor.matmul_mx(
+                    out=banks[s][c][:],
+                    lhsT=w4c[:, b, 2 * c * P : 2 * (c + 1) * P].bitcast(FP4X4),
+                    lhsT_scale=w4s[:, b, :].bitcast(U8)[:, c * P : (c + 1) * P],
+                    rhs=hcodes[b][s][:].bitcast(FP8X4),
+                    rhs_scale=hscale[b][s][:],
+                    start=(b == 0),
+                    stop=(b == HB - 1),
+                )
+
+        def gather_g(c, s):
+            nc.vector.tensor_copy(gpick[c][s][:], gwin[c][:].indirect(offs_of(s)))
+
+        def finish(c, s):
+            nc.vector.tensor_tensor(out=diff[c][s][:], in0=banks[s][c][:], in1=gpick[c][s][:], op=ALU.subtract)
+            nc.scalar.activation(out=diff[c][s][:], in_=diff[c][s][:], func=ACT.Abs, scale=weight[:, c : c + 1])
+            nc.sync.dma_start(out=out[c * P : (c + 1) * P, s * TOK : (s + 1) * TOK], in_=diff[c][s][:])
+
+        nc.sync.dma_start(offsets[:], offs)
+        nc.vector.memset(tscale[:], 0)
+        nc.vector.memset(w4s[:], 0)
+        for q in range(4):
+            nc.gpsimd.dma_start(
+                out=tscale[32 * q : 32 * q + 4 * KA, :],
+                in_=tab_scales[:, 4 * q : 4 * q + 4, :].bitcast(I32),
+            )
+        load_w1(0, 0)
+        load_words(0)
+        nc.sync.dma_start(out=bias[:], in_=b1.rearrange("(b p t) -> p b t", b=HB, t=PACK))
+        load_w1(0, 1)
+        load_words(1)
+        load_w1(0, 2)
+        load_words(2)
+        load_w1(1, 0)
+        nc.sync.dma_start(out=w4c[:].bitcast(I32), in_=w4_words.rearrange("a p n -> p a n").bitcast(I32))
+        load_w1(1, 1)
+        for q in range(4):
+            nc.sync.dma_start(
+                out=w4s[32 * q : 32 * q + 4, :, :],
+                in_=w4_scales[:, 4 * q : 4 * q + 4, :].rearrange("a r n -> r a n").bitcast(I32),
+            )
+        load_w1(1, 2)
+        with nc.allow_non_contiguous_dma(reason="one weight a partition"):
+            nc.sync.dma_start(out=weight[:], in_=wgt.rearrange("(c p) -> p c", p=P))
+        for c in range(NC):
+            nc.sync.dma_start(out=gwin[c][:], in_=gT[c * P : (c + 1) * P, :])
+
+        cast_w1(0, 0, 0, 64, "S")
+        cast_w1(0, 0, 64, 128, "V")
+        gather_scales(0)
+        quant_w1(0, 0)
+        gather_scales(1)
+        for a in range(KA):
+            if a > 0:
+                cast_w1(0, a, 0, 128, "S")
+            gather_words(a, 0)
+            if a > 0:
+                quant_w1(0, a)
+            mm1(0, a, 0)
+            gather_words(a, 1)
+            mm1(0, a, 1)
+        cast_w1(1, 0, 0, 128, "V")
+        evac_h(0, 0)
+        quant_w1(1, 0)
+        evac_h(0, 1)
+        weave_h(0, 0, 0, 128, "V")
+        mm1(1, 0, 0)
+        mm1(1, 0, 1)
+        cast_w1(1, 1, 0, 48, "S")
+        cast_w1(1, 1, 48, 128, "V")
+        quant_h(0, 0)
+        quant_w1(1, 1)
+        mm1(1, 1, 0)
+        mm1(1, 1, 1)
+        weave_h(0, 1, 0, 128, "V")
+        cast_w1(1, 2, 0, 64, "S")
+        cast_w1(1, 2, 64, 128, "V")
+        quant_h(0, 1)
+        quant_w1(1, 2)
+        mm1(1, 2, 0)
+        mm1(1, 2, 1)
+        evac_h(1, 0)
+        mm2(0, 0)
+        gather_g(0, 0)
+        gather_g(0, 1)
+        weave_h(1, 0, 0, 128, "V")
+        evac_h(1, 1)
+        mm2(0, 1)
+        gather_g(1, 0)
+        quant_h(1, 0)
+        mm2(1, 0)
+        weave_h(1, 1, 0, 128, "S")
+        gather_g(1, 1)
+        finish(0, 0)
+        finish(1, 0)
+        gather_g(2, 0)
+        quant_h(1, 1)
+        mm2(1, 1)
+        finish(2, 0)
+        gather_g(3, 0)
+        finish(0, 1)
+        finish(3, 0)
+        finish(1, 1)
+        gather_g(2, 1)
+        finish(2, 1)
+        gather_g(3, 1)
+        finish(3, 1)

@@ -68,6 +68,11 @@ def tile_list_flow_anomaly_residuals_kernel(tc, tab_words, tab_scales, offs, w1,
         def load_words(a):
             nc.sync.dma_start(out=words[a][:], in_=tab_words[a].rearrange("p t i -> p (t i)").bitcast(I32))
 
+        def load_tscale(first, last):
+            for a, q in [divmod(i, 4) for i in range(first, last)]:
+                row = 32 * q + 4 * a
+                nc.sync.dma_start(out=tscale[row : row + 4, :], in_=tab_scales[a, 4 * q : 4 * q + 4, :].bitcast(I32))
+
         def cast_w1(b, a, m0, m1, eng):
             dst = wbf[b][a][:].rearrange("p (t m j) -> p m j t", t=PACK, j=PACK)[:, m0:m1]
             src = raw[b][a][:].rearrange("p j (m t) -> p m j t", t=PACK)[:, m0:m1]
@@ -134,89 +139,96 @@ def tile_list_flow_anomaly_residuals_kernel(tc, tab_words, tab_scales, offs, w1,
             nc.sync.dma_start(out=out[c * P : (c + 1) * P, s * TOK : (s + 1) * TOK], in_=diff[c][s][:])
 
         nc.sync.dma_start(offsets[:], offs)
-        nc.vector.memset(tscale[:], 0)
-        nc.vector.memset(w4s[:], 0)
-        for q in range(4):
-            nc.gpsimd.dma_start(
-                out=tscale[32 * q : 32 * q + 4 * KA, :],
-                in_=tab_scales[:, 4 * q : 4 * q + 4, :].bitcast(I32),
-            )
-        load_w1(0, 0)
+        nc.gpsimd.memset(tscale[:], 0)
+        nc.gpsimd.memset(w4s[:], 0)
         load_words(0)
+        load_tscale(0, 6)
+        load_words(1)
+        load_tscale(6, 12)
+        load_w1(0, 0)
         nc.sync.dma_start(out=bias[:], in_=b1.rearrange("(b p t) -> p b t", b=HB, t=PACK))
         load_w1(0, 1)
-        load_words(1)
         load_w1(0, 2)
         load_words(2)
         load_w1(1, 0)
-        nc.sync.dma_start(out=w4c[:].bitcast(I32), in_=w4_words.rearrange("a p n -> p a n").bitcast(I32))
         load_w1(1, 1)
+        load_w1(1, 2)
+        nc.sync.dma_start(out=w4c[:].bitcast(I32), in_=w4_words.rearrange("a p n -> p a n").bitcast(I32))
         for q in range(4):
             nc.sync.dma_start(
                 out=w4s[32 * q : 32 * q + 4, :, :],
                 in_=w4_scales[:, 4 * q : 4 * q + 4, :].rearrange("a r n -> r a n").bitcast(I32),
             )
-        load_w1(1, 2)
+        nc.sync.dma_start(out=gwin[0][:], in_=gT[0 * P : (0 + 1) * P, :])
         with nc.allow_non_contiguous_dma(reason="one weight a partition"):
             nc.sync.dma_start(out=weight[:], in_=wgt.rearrange("(c p) -> p c", p=P))
-        for c in range(NC):
-            nc.sync.dma_start(out=gwin[c][:], in_=gT[c * P : (c + 1) * P, :])
-
-        cast_w1(0, 0, 0, 64, "S")
-        cast_w1(0, 0, 64, 128, "V")
+        nc.sync.dma_start(out=gwin[1][:], in_=gT[1 * P : (1 + 1) * P, :])
+        nc.sync.dma_start(out=gwin[2][:], in_=gT[2 * P : (2 + 1) * P, :])
+        nc.sync.dma_start(out=gwin[3][:], in_=gT[3 * P : (3 + 1) * P, :])
+        gather_words(0, 0)
+        gather_words(0, 1)
+        gather_words(1, 0)
+        gather_words(1, 1)
+        cast_w1(0, 0, 0, 112, "S")
+        cast_w1(0, 0, 112, 128, "V")
         gather_scales(0)
-        quant_w1(0, 0)
         gather_scales(1)
-        for a in range(KA):
-            if a > 0:
-                cast_w1(0, a, 0, 128, "S")
-            gather_words(a, 0)
-            if a > 0:
-                quant_w1(0, a)
-            mm1(0, a, 0)
-            gather_words(a, 1)
-            mm1(0, a, 1)
-        cast_w1(1, 0, 0, 128, "V")
+        cast_w1(0, 1, 0, 48, "S")
+        cast_w1(0, 1, 48, 128, "V")
+        quant_w1(0, 0)
+        quant_w1(0, 1)
+        mm1(0, 0, 0)
+        mm1(0, 0, 1)
+        cast_w1(0, 2, 0, 128, "V")
+        quant_w1(0, 2)
+        mm1(0, 1, 0)
+        gather_words(2, 0)
+        mm1(0, 2, 0)
+        mm1(0, 1, 1)
+        gather_words(2, 1)
+        mm1(0, 2, 1)
         evac_h(0, 0)
+        cast_w1(1, 0, 0, 16, "S")
+        cast_w1(1, 0, 16, 128, "V")
         quant_w1(1, 0)
         evac_h(0, 1)
+        cast_w1(1, 1, 0, 32, "S")
+        cast_w1(1, 1, 32, 128, "V")
         weave_h(0, 0, 0, 128, "V")
         mm1(1, 0, 0)
-        mm1(1, 0, 1)
-        cast_w1(1, 1, 0, 48, "S")
-        cast_w1(1, 1, 48, 128, "V")
-        quant_h(0, 0)
-        quant_w1(1, 1)
-        mm1(1, 1, 0)
-        mm1(1, 1, 1)
-        weave_h(0, 1, 0, 128, "V")
         cast_w1(1, 2, 0, 64, "S")
         cast_w1(1, 2, 64, 128, "V")
-        quant_h(0, 1)
+        quant_w1(1, 1)
+        mm1(1, 1, 0)
+        quant_h(0, 0)
         quant_w1(1, 2)
         mm1(1, 2, 0)
+        mm1(1, 0, 1)
+        mm1(1, 1, 1)
         mm1(1, 2, 1)
+        weave_h(0, 1, 0, 128, "S")
         evac_h(1, 0)
         mm2(0, 0)
-        gather_g(0, 0)
-        gather_g(0, 1)
-        weave_h(1, 0, 0, 128, "V")
-        evac_h(1, 1)
-        mm2(0, 1)
-        gather_g(1, 0)
+        quant_h(0, 1)
+        weave_h(1, 0, 0, 128, "S")
         quant_h(1, 0)
         mm2(1, 0)
+        evac_h(1, 1)
+        mm2(0, 1)
         weave_h(1, 1, 0, 128, "S")
-        gather_g(1, 1)
-        finish(0, 0)
-        finish(1, 0)
-        gather_g(2, 0)
         quant_h(1, 1)
         mm2(1, 1)
+        gather_g(0, 0)
+        finish(0, 0)
+        gather_g(1, 0)
+        finish(1, 0)
+        gather_g(2, 0)
         finish(2, 0)
         gather_g(3, 0)
-        finish(0, 1)
         finish(3, 0)
+        gather_g(0, 1)
+        finish(0, 1)
+        gather_g(1, 1)
         finish(1, 1)
         gather_g(2, 1)
         finish(2, 1)

@@ -40,22 +40,23 @@ def tile_list_flow_anomaly_residuals_kernel(tc, tab_words, tab_scales, offs, w1,
         vcodes = [[keep.tile([P, TOK], I32, name=f"vcodes{a}_{s}", align_bytes=64) for s in range(SH)] for a in range(KA)]
         vscale = [keep.tile([P, TOK], U8, name=f"vscale{s}", align_bytes=64) for s in range(SH)]
         raw = [[keep.tile([P, PACK, KP], F32, name=f"raw{b}_{a}", align_bytes=64) for a in range(KA)] for b in range(HB)]
-        wbf3 = [keep.tile([P, PACK * KP], BF16, name=f"wbf{a}", align_bytes=64) for a in range(KA)]
-        wbf = [wbf3 for b in range(HB)]
+        wbf = {}
         wcodes = [[keep.tile([P, KP], U32, name=f"wcodes{b}_{a}", align_bytes=64) for a in range(KA)] for b in range(HB)]
         wscale = [[keep.tile([P, KP], U8, name=f"wscale{b}_{a}", align_bytes=64) for a in range(KA)] for b in range(HB)]
         bias = keep.tile([P, HB, PACK], F32, name="bias")
         weight = keep.tile([P, NC], F32, name="weight")
         w4c = keep.tile([P, HB, 2 * N], U8, name="w4c", align_bytes=64)
         w4s = keep.tile([P, HB, N // 4], I32, name="w4s", align_bytes=64)
-        gwin = [keep.tile([P, T], F32, name=f"gwin{c}", align_bytes=64) for c in range(NC)]
-        gpick = [[keep.tile([P, TOK], F32, name=f"gpick{c}_{s}", align_bytes=64) for s in range(SH)] for c in range(NC)]
+        gwin = [keep.tile([P, T], F32, name=f"gwin{c}", tag=f"gwin{c}", align_bytes=64) for c in range(NC)]
+        gpick = [[keep.tile([P, TOK], F32, name=f"gpick{c}_{s}", tag=f"gpick{c}_{s}", align_bytes=64) for s in range(SH)] for c in range(NC)]
         hrow = [[keep.tile([P, PACK, TOK], BF16, name=f"hrow{b}_{s}", align_bytes=64) for s in range(SH)] for b in range(HB)]
         hint2 = [keep.tile([P, PACK * TOK], BF16, name=f"hint{s}", align_bytes=64) for s in range(SH)]
         hint = [hint2 for b in range(HB)]
-        hcodes = [[keep.tile([P, TOK], U32, name=f"hcodes{b}_{s}", align_bytes=64) for s in range(SH)] for b in range(HB)]
+        hcodes = {}
+        hcodes_home = {(0, 0): "wbf2", (0, 1): "gwin0", (1, 0): "gwin2", (1, 1): "gpick0_0"}
         hscale = [[keep.tile([P, TOK], U8, name=f"hscale{b}_{s}", align_bytes=64) for s in range(SH)] for b in range(HB)]
-        diff = [[keep.tile([P, TOK], F32, name=f"diff{c}_{s}", align_bytes=64) for s in range(SH)] for c in range(NC)]
+        diff = {}
+        diff_home = {0: "gwin3", 1: "diff1"}
         banks = [[psum.tile([P, TOK], F32, name=f"bank{s}_{t}") for t in range(PACK)] for s in range(SH)]
 
         def offs_of(s):
@@ -74,7 +75,9 @@ def tile_list_flow_anomaly_residuals_kernel(tc, tab_words, tab_scales, offs, w1,
                 nc.sync.dma_start(out=tscale[row : row + 4, :], in_=tab_scales[a, 4 * q : 4 * q + 4, :].bitcast(I32))
 
         def cast_w1(b, a, m0, m1, eng):
-            dst = wbf[b][a][:].rearrange("p (t m j) -> p m j t", t=PACK, j=PACK)[:, m0:m1]
+            if m0 == 0:
+                wbf[b, a] = keep.tile([P, PACK * KP], BF16, name=f"wbf{b}_{a}", tag=f"wbf{a}", align_bytes=64)
+            dst = wbf[b, a][:].rearrange("p (t m j) -> p m j t", t=PACK, j=PACK)[:, m0:m1]
             src = raw[b][a][:].rearrange("p j (m t) -> p m j t", t=PACK)[:, m0:m1]
             if eng == "V":
                 nc.vector.tensor_copy(out=dst, in_=src)
@@ -82,7 +85,7 @@ def tile_list_flow_anomaly_residuals_kernel(tc, tab_words, tab_scales, offs, w1,
                 nc.scalar.copy(out=dst, in_=src)
 
         def quant_w1(b, a):
-            nc.vector.quantize_mx(out=wcodes[b][a][:].bitcast(FP8X4), scales=wscale[b][a][:], in_=wbf[b][a][:])
+            nc.vector.quantize_mx(out=wcodes[b][a][:].bitcast(FP8X4), scales=wscale[b][a][:], in_=wbf[b, a][:])
 
         def gather_words(a, s):
             nc.vector.tensor_copy(vcodes[a][s][:].bitcast(U32), words[a][:].bitcast(U32).indirect(offs_of(s)))
@@ -116,7 +119,8 @@ def tile_list_flow_anomaly_residuals_kernel(tc, tab_words, tab_scales, offs, w1,
                 nc.scalar.copy(out=dst, in_=src)
 
         def quant_h(b, s):
-            nc.vector.quantize_mx(out=hcodes[b][s][:].bitcast(FP8X4), scales=hscale[b][s][:], in_=hint[b][s][:])
+            hcodes[b, s] = keep.tile([P, TOK], U32, name=f"hcodes{b}_{s}", tag=hcodes_home[b, s], align_bytes=64)
+            nc.vector.quantize_mx(out=hcodes[b, s][:].bitcast(FP8X4), scales=hscale[b][s][:], in_=hint[b][s][:])
 
         def mm2(b, s):
             for c in range(NC):
@@ -124,7 +128,7 @@ def tile_list_flow_anomaly_residuals_kernel(tc, tab_words, tab_scales, offs, w1,
                     out=banks[s][c][:],
                     lhsT=w4c[:, b, 2 * c * P : 2 * (c + 1) * P].bitcast(FP4X4),
                     lhsT_scale=w4s[:, b, :].bitcast(U8)[:, c * P : (c + 1) * P],
-                    rhs=hcodes[b][s][:].bitcast(FP8X4),
+                    rhs=hcodes[b, s][:].bitcast(FP8X4),
                     rhs_scale=hscale[b][s][:],
                     start=(b == 0),
                     stop=(b == HB - 1),
@@ -133,10 +137,13 @@ def tile_list_flow_anomaly_residuals_kernel(tc, tab_words, tab_scales, offs, w1,
         def gather_g(c, s):
             nc.vector.tensor_copy(gpick[c][s][:], gwin[c][:].indirect(offs_of(s)))
 
-        def finish(c, s):
-            nc.vector.tensor_tensor(out=diff[c][s][:], in0=banks[s][c][:], in1=gpick[c][s][:], op=ALU.subtract)
-            nc.scalar.activation(out=diff[c][s][:], in_=diff[c][s][:], func=ACT.Abs, scale=weight[:, c : c + 1])
-            nc.sync.dma_start(out=out[c * P : (c + 1) * P, s * TOK : (s + 1) * TOK], in_=diff[c][s][:])
+        def finish(c, s, j0, j1):
+            if s not in diff:
+                diff[s] = keep.tile([P, NC, TOK], F32, name=f"diff{s}", tag=diff_home[s], align_bytes=64)
+            d = diff[s][:, c, j0:j1]
+            nc.vector.tensor_tensor(out=d, in0=banks[s][c][:, j0:j1], in1=gpick[c][s][:, j0:j1], op=ALU.subtract)
+            nc.scalar.activation(out=d, in_=d, func=ACT.Abs, scale=weight[:, c : c + 1])
+            nc.sync.dma_start(out=out[c * P : (c + 1) * P, s * TOK + j0 : s * TOK + j1], in_=d)
 
         nc.sync.dma_start(offsets[:], offs)
         nc.gpsimd.memset(tscale[:], 0)
@@ -169,68 +176,66 @@ def tile_list_flow_anomaly_residuals_kernel(tc, tab_words, tab_scales, offs, w1,
         gather_words(0, 1)
         gather_words(1, 0)
         gather_words(1, 1)
-        cast_w1(0, 0, 0, 112, "S")
-        cast_w1(0, 0, 112, 128, "V")
+        cast_w1(0, 0, 0, 128, "S")
         gather_scales(0)
         gather_scales(1)
-        cast_w1(0, 1, 0, 48, "S")
-        cast_w1(0, 1, 48, 128, "V")
         quant_w1(0, 0)
-        quant_w1(0, 1)
         mm1(0, 0, 0)
         mm1(0, 0, 1)
-        cast_w1(0, 2, 0, 128, "V")
-        quant_w1(0, 2)
+        cast_w1(0, 1, 0, 64, "S")
+        cast_w1(0, 1, 64, 128, "V")
+        quant_w1(0, 1)
         mm1(0, 1, 0)
+        mm1(0, 1, 1)
+        cast_w1(0, 2, 0, 64, "S")
+        cast_w1(0, 2, 64, 128, "V")
+        quant_w1(0, 2)
         gather_words(2, 0)
         mm1(0, 2, 0)
-        mm1(0, 1, 1)
         gather_words(2, 1)
         mm1(0, 2, 1)
         evac_h(0, 0)
-        cast_w1(1, 0, 0, 16, "S")
-        cast_w1(1, 0, 16, 128, "V")
-        quant_w1(1, 0)
         evac_h(0, 1)
-        cast_w1(1, 1, 0, 32, "S")
-        cast_w1(1, 1, 32, 128, "V")
-        weave_h(0, 0, 0, 128, "V")
+        cast_w1(1, 0, 0, 128, "V")
+        quant_w1(1, 0)
         mm1(1, 0, 0)
-        cast_w1(1, 2, 0, 64, "S")
-        cast_w1(1, 2, 64, 128, "V")
+        mm1(1, 0, 1)
+        cast_w1(1, 1, 0, 128, "V")
         quant_w1(1, 1)
         mm1(1, 1, 0)
-        quant_h(0, 0)
+        cast_w1(1, 2, 0, 128, "V")
         quant_w1(1, 2)
         mm1(1, 2, 0)
-        mm1(1, 0, 1)
         mm1(1, 1, 1)
         mm1(1, 2, 1)
+        weave_h(0, 0, 0, 128, "S")
+        quant_h(0, 0)
         weave_h(0, 1, 0, 128, "S")
+        gather_g(0, 0)
+        gather_g(0, 1)
+        quant_h(0, 1)
         evac_h(1, 0)
         mm2(0, 0)
-        quant_h(0, 1)
         weave_h(1, 0, 0, 128, "S")
-        quant_h(1, 0)
-        mm2(1, 0)
         evac_h(1, 1)
         mm2(0, 1)
         weave_h(1, 1, 0, 128, "S")
+        gather_g(1, 0)
+        gather_g(1, 1)
+        gather_g(2, 0)
+        gather_g(2, 1)
+        quant_h(1, 0)
+        mm2(1, 0)
+        gather_g(3, 0)
+        gather_g(3, 1)
+        finish(0, 0, 0, TOK)
+        finish(1, 0, 0, TOK)
         quant_h(1, 1)
         mm2(1, 1)
-        gather_g(0, 0)
-        finish(0, 0)
-        gather_g(1, 0)
-        finish(1, 0)
-        gather_g(2, 0)
-        finish(2, 0)
-        gather_g(3, 0)
-        finish(3, 0)
-        gather_g(0, 1)
-        finish(0, 1)
-        gather_g(1, 1)
-        finish(1, 1)
-        gather_g(2, 1)
-        finish(2, 1)
-        gather_g(3, 1)
-        finish(3, 1)
+        finish(2, 0, 0, TOK)
+        finish(3, 0, 0, TOK)
+        finish(0, 1, 0, TOK)
+        finish(1, 1, 0, TOK)
+        finish(2, 1, 0, TOK)
+        finish(3, 1, 0, 256)
+        finish(3, 1, 256, TOK)

@@ -37,8 +37,8 @@ def tile_list_flow_anomaly_residuals_kernel(tc, tab_words, tab_scales, offs, w1,
         offsets = lists.tile([P, S // 16], U16, name="offsets")
         words = [keep.tile([P, T], I32, name=f"words{a}", align_bytes=64) for a in range(KA)]
         tscale = keep.tile([P, T // 4], I32, name="tscale", align_bytes=64)
-        vcodes = [[keep.tile([P, TOK], I32, name=f"vcodes{a}_{s}", align_bytes=64) for s in range(SH)] for a in range(KA)]
-        vscale = [keep.tile([P, TOK], U8, name=f"vscale{s}", align_bytes=64) for s in range(SH)]
+        vcodes = [keep.tile([P, S], I32, name=f"vcodes{a}", align_bytes=64) for a in range(KA)]
+        vscale = keep.tile([P, S], U8, name="vscale", align_bytes=64)
         raw = [[keep.tile([P, PACK, KP], F32, name=f"raw{b}_{a}", align_bytes=64) for a in range(KA)] for b in range(HB)]
         wbf = {}
         wcodes = [[keep.tile([P, KP], U32, name=f"wcodes{b}_{a}", align_bytes=64) for a in range(KA)] for b in range(HB)]
@@ -48,19 +48,19 @@ def tile_list_flow_anomaly_residuals_kernel(tc, tab_words, tab_scales, offs, w1,
         w4c = keep.tile([P, HB, 2 * N], U8, name="w4c", align_bytes=64)
         w4s = keep.tile([P, HB, N // 4], I32, name="w4s", align_bytes=64)
         gwin = [keep.tile([P, T], F32, name=f"gwin{c}", tag=f"gwin{c}", align_bytes=64) for c in range(NC)]
-        gpick = [[keep.tile([P, TOK], F32, name=f"gpick{c}_{s}", tag=f"gpick{c}_{s}", align_bytes=64) for s in range(SH)] for c in range(NC)]
+        gpick0 = [keep.tile([P, TOK], F32, name=f"gpick0_{s}", tag=f"gpick0_{s}", align_bytes=64) for s in range(SH)]
+        gpick = [None] + [keep.tile([P, S], F32, name=f"gpick{c}", align_bytes=64) for c in range(1, NC)]
         hrow = [[keep.tile([P, PACK, TOK], BF16, name=f"hrow{b}_{s}", align_bytes=64) for s in range(SH)] for b in range(HB)]
-        hint2 = [keep.tile([P, PACK * TOK], BF16, name=f"hint{s}", align_bytes=64) for s in range(SH)]
-        hint = [hint2 for b in range(HB)]
+        hint = [[keep.tile([P, PACK * TOK], BF16, name=f"hint{b}_{s}", align_bytes=64) for s in range(SH)] for b in range(HB)]
         hcodes = {}
-        hcodes_home = {(0, 0): "wbf2", (0, 1): "gwin0", (1, 0): "gwin2", (1, 1): "gpick0_0"}
+        hcodes_home = {(0, 0): "gwin0", (0, 1): "gwin1", (1, 0): "gwin2", (1, 1): "gpick0_0"}
         hscale = [[keep.tile([P, TOK], U8, name=f"hscale{b}_{s}", align_bytes=64) for s in range(SH)] for b in range(HB)]
         diff = {}
         diff_home = {0: "gwin3", 1: "diff1"}
         banks = [[psum.tile([P, TOK], F32, name=f"bank{s}_{t}") for t in range(PACK)] for s in range(SH)]
 
-        def offs_of(s):
-            return offsets[:, s * OC : (s + 1) * OC]
+        def offs_of(j0, j1):
+            return offsets[:, j0 // 16 : j1 // 16]
 
         def load_w1(b, a):
             src = w1[a * KP : (a + 1) * KP, b * KP : (b + 1) * KP]
@@ -70,9 +70,8 @@ def tile_list_flow_anomaly_residuals_kernel(tc, tab_words, tab_scales, offs, w1,
             nc.sync.dma_start(out=words[a][:], in_=tab_words[a].rearrange("p t i -> p (t i)").bitcast(I32))
 
         def load_tscale(first, last):
-            for a, q in [divmod(i, 4) for i in range(first, last)]:
-                row = 32 * q + 4 * a
-                nc.sync.dma_start(out=tscale[row : row + 4, :], in_=tab_scales[a, 4 * q : 4 * q + 4, :].bitcast(I32))
+            for a, r in [divmod(i, 4) for i in range(first, last)]:
+                nc.sync.dma_start(out=tscale[4 * a + r : P : 32, :], in_=tab_scales[a, r:16:4, :].bitcast(I32))
 
         def cast_w1(b, a, m0, m1, eng):
             if m0 == 0:
@@ -87,11 +86,11 @@ def tile_list_flow_anomaly_residuals_kernel(tc, tab_words, tab_scales, offs, w1,
         def quant_w1(b, a):
             nc.vector.quantize_mx(out=wcodes[b][a][:].bitcast(FP8X4), scales=wscale[b][a][:], in_=wbf[b, a][:])
 
-        def gather_words(a, s):
-            nc.vector.tensor_copy(vcodes[a][s][:].bitcast(U32), words[a][:].bitcast(U32).indirect(offs_of(s)))
+        def gather_words(a, j0, j1):
+            nc.vector.tensor_copy(vcodes[a][:, j0:j1].bitcast(U32), words[a][:].bitcast(U32).indirect(offs_of(j0, j1)))
 
-        def gather_scales(s):
-            nc.vector.tensor_copy(vscale[s][:], tscale[:].bitcast(U8).indirect(offs_of(s)))
+        def gather_scales():
+            nc.vector.tensor_copy(vscale[:], tscale[:].bitcast(U8).indirect(offs_of(0, S)))
 
         def mm1(b, a, s):
             for t in range(PACK):
@@ -100,8 +99,8 @@ def tile_list_flow_anomaly_residuals_kernel(tc, tab_words, tab_scales, offs, w1,
                     out=banks[s][t][:],
                     lhsT=wcodes[b][a][:, cols].bitcast(FP8X4),
                     lhsT_scale=wscale[b][a][:, cols],
-                    rhs=vcodes[a][s][:].bitcast(FP8X4),
-                    rhs_scale=vscale[s][PACK * a : P, :],
+                    rhs=vcodes[a][:, s * TOK : (s + 1) * TOK].bitcast(FP8X4),
+                    rhs_scale=vscale[PACK * a : P, s * TOK : (s + 1) * TOK],
                     start=(a == 0),
                     stop=(a == KA - 1),
                 )
@@ -134,14 +133,19 @@ def tile_list_flow_anomaly_residuals_kernel(tc, tab_words, tab_scales, offs, w1,
                     stop=(b == HB - 1),
                 )
 
-        def gather_g(c, s):
-            nc.vector.tensor_copy(gpick[c][s][:], gwin[c][:].indirect(offs_of(s)))
+        def picked(c, j0, j1):
+            if c == 0:
+                return gpick0[j0 // TOK][:, j0 % TOK : j0 % TOK + j1 - j0]
+            return gpick[c][:, j0:j1]
+
+        def gather_g(c, j0, j1):
+            nc.vector.tensor_copy(picked(c, j0, j1), gwin[c][:].indirect(offs_of(j0, j1)))
 
         def finish(c, s, j0, j1):
             if s not in diff:
                 diff[s] = keep.tile([P, NC, TOK], F32, name=f"diff{s}", tag=diff_home[s], align_bytes=64)
             d = diff[s][:, c, j0:j1]
-            nc.vector.tensor_tensor(out=d, in0=banks[s][c][:, j0:j1], in1=gpick[c][s][:, j0:j1], op=ALU.subtract)
+            nc.vector.tensor_tensor(out=d, in0=banks[s][c][:, j0:j1], in1=picked(c, s * TOK + j0, s * TOK + j1), op=ALU.subtract)
             nc.scalar.activation(out=d, in_=d, func=ACT.Abs, scale=weight[:, c : c + 1])
             nc.sync.dma_start(out=out[c * P : (c + 1) * P, s * TOK + j0 : s * TOK + j1], in_=d)
 
@@ -160,25 +164,22 @@ def tile_list_flow_anomaly_residuals_kernel(tc, tab_words, tab_scales, offs, w1,
         load_w1(1, 0)
         load_w1(1, 1)
         load_w1(1, 2)
-        nc.sync.dma_start(out=w4c[:].bitcast(I32), in_=w4_words.rearrange("a p n -> p a n").bitcast(I32))
-        for q in range(4):
-            nc.sync.dma_start(
-                out=w4s[32 * q : 32 * q + 4, :, :],
-                in_=w4_scales[:, 4 * q : 4 * q + 4, :].rearrange("a r n -> r a n").bitcast(I32),
-            )
         nc.sync.dma_start(out=gwin[0][:], in_=gT[0 * P : (0 + 1) * P, :])
-        with nc.allow_non_contiguous_dma(reason="one weight a partition"):
-            nc.sync.dma_start(out=weight[:], in_=wgt.rearrange("(c p) -> p c", p=P))
         nc.sync.dma_start(out=gwin[1][:], in_=gT[1 * P : (1 + 1) * P, :])
         nc.sync.dma_start(out=gwin[2][:], in_=gT[2 * P : (2 + 1) * P, :])
+        nc.sync.dma_start(out=w4c[:].bitcast(I32), in_=w4_words.rearrange("a p n -> p a n").bitcast(I32))
+        for r in range(4):
+            nc.sync.dma_start(
+                out=w4s[r:P:32, :, :],
+                in_=w4_scales[:, r:16:4, :].rearrange("a q n -> q a n").bitcast(I32),
+            )
         nc.sync.dma_start(out=gwin[3][:], in_=gT[3 * P : (3 + 1) * P, :])
-        gather_words(0, 0)
-        gather_words(0, 1)
-        gather_words(1, 0)
-        gather_words(1, 1)
+        with nc.allow_non_contiguous_dma(reason="one weight a partition"):
+            nc.sync.dma_start(out=weight[:], in_=wgt.rearrange("(c p) -> p c", p=P))
+        gather_words(0, 0, S)
+        gather_words(1, 0, S)
         cast_w1(0, 0, 0, 128, "S")
-        gather_scales(0)
-        gather_scales(1)
+        gather_scales()
         quant_w1(0, 0)
         mm1(0, 0, 0)
         mm1(0, 0, 1)
@@ -190,9 +191,9 @@ def tile_list_flow_anomaly_residuals_kernel(tc, tab_words, tab_scales, offs, w1,
         cast_w1(0, 2, 0, 64, "S")
         cast_w1(0, 2, 64, 128, "V")
         quant_w1(0, 2)
-        gather_words(2, 0)
+        gather_words(2, 0, TOK)
         mm1(0, 2, 0)
-        gather_words(2, 1)
+        gather_words(2, TOK, S)
         mm1(0, 2, 1)
         evac_h(0, 0)
         evac_h(0, 1)
@@ -209,10 +210,11 @@ def tile_list_flow_anomaly_residuals_kernel(tc, tab_words, tab_scales, offs, w1,
         mm1(1, 1, 1)
         mm1(1, 2, 1)
         weave_h(0, 0, 0, 128, "S")
-        quant_h(0, 0)
         weave_h(0, 1, 0, 128, "S")
-        gather_g(0, 0)
-        gather_g(0, 1)
+        gather_g(0, 0, TOK)
+        gather_g(0, TOK, S)
+        quant_h(0, 0)
+        gather_g(1, 0, S)
         quant_h(0, 1)
         evac_h(1, 0)
         mm2(0, 0)
@@ -220,18 +222,14 @@ def tile_list_flow_anomaly_residuals_kernel(tc, tab_words, tab_scales, offs, w1,
         evac_h(1, 1)
         mm2(0, 1)
         weave_h(1, 1, 0, 128, "S")
-        gather_g(1, 0)
-        gather_g(1, 1)
-        gather_g(2, 0)
-        gather_g(2, 1)
+        gather_g(2, 0, S)
         quant_h(1, 0)
         mm2(1, 0)
-        gather_g(3, 0)
-        gather_g(3, 1)
+        gather_g(3, 0, S)
         finish(0, 0, 0, TOK)
-        finish(1, 0, 0, TOK)
         quant_h(1, 1)
         mm2(1, 1)
+        finish(1, 0, 0, TOK)
         finish(2, 0, 0, TOK)
         finish(3, 0, 0, TOK)
         finish(0, 1, 0, TOK)

@@ -51,10 +51,9 @@ def tile_list_flow_anomaly_residuals_kernel(tc, tab_words, tab_scales, offs, w1,
         gpick0 = [keep.tile([P, TOK], F32, name=f"gpick0_{s}", tag=f"gpick0_{s}", align_bytes=64) for s in range(SH)]
         gpick = [None] + [keep.tile([P, S], F32, name=f"gpick{c}", align_bytes=64) for c in range(1, NC)]
         hrow = [[keep.tile([P, PACK, TOK], BF16, name=f"hrow{b}_{s}", align_bytes=64) for s in range(SH)] for b in range(HB)]
-        hint = [[keep.tile([P, PACK * TOK], BF16, name=f"hint{b}_{s}", align_bytes=64) for s in range(SH)] for b in range(HB)]
+        hint = [keep.tile([P, PACK * S], BF16, name=f"hint{b}", align_bytes=64) for b in range(HB)]
         hcodes = {}
-        hcodes_home = {(0, 0): "gwin0", (0, 1): "gwin1", (1, 0): "gwin2", (1, 1): "gpick0_0"}
-        hscale = [[keep.tile([P, TOK], U8, name=f"hscale{b}_{s}", align_bytes=64) for s in range(SH)] for b in range(HB)]
+        hscale = [keep.tile([P, S], U8, name=f"hscale{b}", align_bytes=64) for b in range(HB)]
         diff = {}
         diff_home = {0: "gwin3", 1: "diff1"}
         banks = [[psum.tile([P, TOK], F32, name=f"bank{s}_{t}") for t in range(PACK)] for s in range(SH)]
@@ -110,16 +109,18 @@ def tile_list_flow_anomaly_residuals_kernel(tc, tab_words, tab_scales, offs, w1,
                 nc.scalar.activation(out=hrow[b][s][:, t, :], in_=banks[s][t][:], func=ACT.Relu, bias=bias[:, b, t : t + 1])
 
         def weave_h(b, s, c0, c1, eng):
-            dst = hint[b][s][:].rearrange("p (c i t) -> p c t i", i=4, t=PACK)[:, c0:c1]
+            dst = hint[b][:, s * PACK * TOK : (s + 1) * PACK * TOK].rearrange("p (c i t) -> p c t i", i=4, t=PACK)[:, c0:c1]
             src = hrow[b][s][:].rearrange("p t (c i) -> p c t i", i=4)[:, c0:c1]
             if eng == "V":
                 nc.vector.tensor_copy(out=dst, in_=src)
             else:
                 nc.scalar.copy(out=dst, in_=src)
 
-        def quant_h(b, s):
-            hcodes[b, s] = keep.tile([P, TOK], U32, name=f"hcodes{b}_{s}", tag=hcodes_home[b, s], align_bytes=64)
-            nc.vector.quantize_mx(out=hcodes[b, s][:].bitcast(FP8X4), scales=hscale[b][s][:], in_=hint[b][s][:])
+        def quant_h(b, j0, j1, home):
+            codes = keep.tile([P, j1 - j0], U32, name=f"hcodes{b}_{j0}", tag=home, align_bytes=64)
+            nc.vector.quantize_mx(out=codes[:].bitcast(FP8X4), scales=hscale[b][:, j0:j1], in_=hint[b][:, PACK * j0 : PACK * j1])
+            for j in range(j0, j1, TOK):
+                hcodes[b, j // TOK] = codes[:, j - j0 : j - j0 + TOK]
 
         def mm2(b, s):
             for c in range(NC):
@@ -127,8 +128,8 @@ def tile_list_flow_anomaly_residuals_kernel(tc, tab_words, tab_scales, offs, w1,
                     out=banks[s][c][:],
                     lhsT=w4c[:, b, 2 * c * P : 2 * (c + 1) * P].bitcast(FP4X4),
                     lhsT_scale=w4s[:, b, :].bitcast(U8)[:, c * P : (c + 1) * P],
-                    rhs=hcodes[b, s][:].bitcast(FP8X4),
-                    rhs_scale=hscale[b][s][:],
+                    rhs=hcodes[b, s].bitcast(FP8X4),
+                    rhs_scale=hscale[b][:, s * TOK : (s + 1) * TOK],
                     start=(b == 0),
                     stop=(b == HB - 1),
                 )
@@ -213,9 +214,8 @@ def tile_list_flow_anomaly_residuals_kernel(tc, tab_words, tab_scales, offs, w1,
         weave_h(0, 1, 0, 128, "S")
         gather_g(0, 0, TOK)
         gather_g(0, TOK, S)
-        quant_h(0, 0)
         gather_g(1, 0, S)
-        quant_h(0, 1)
+        quant_h(0, 0, S, "gwin1")
         evac_h(1, 0)
         mm2(0, 0)
         weave_h(1, 0, 0, 128, "S")
@@ -223,11 +223,11 @@ def tile_list_flow_anomaly_residuals_kernel(tc, tab_words, tab_scales, offs, w1,
         mm2(0, 1)
         weave_h(1, 1, 0, 128, "S")
         gather_g(2, 0, S)
-        quant_h(1, 0)
+        quant_h(1, 0, TOK, "gwin2")
         mm2(1, 0)
         gather_g(3, 0, S)
         finish(0, 0, 0, TOK)
-        quant_h(1, 1)
+        quant_h(1, TOK, S, "gpick0_0")
         mm2(1, 1)
         finish(1, 0, 0, TOK)
         finish(2, 0, 0, TOK)
@@ -235,5 +235,5 @@ def tile_list_flow_anomaly_residuals_kernel(tc, tab_words, tab_scales, offs, w1,
         finish(0, 1, 0, TOK)
         finish(1, 1, 0, TOK)
         finish(2, 1, 0, TOK)
-        finish(3, 1, 0, 256)
-        finish(3, 1, 256, TOK)
+        finish(3, 1, 0, 384)
+        finish(3, 1, 384, TOK)

@@ -24,7 +24,7 @@ HB = H // KP
 NC = N // P
 TOK = 512
 SH = S // TOK
-OC = TOK // 16
+WIDTH = {F32: 4, I32: 4, U32: 4, BF16: 2, U8: 1}
 
 
 def tile_list_flow_anomaly_residuals_kernel(tc, tab_words, tab_scales, offs, w1, b1, w4_words, w4_scales, gT, wgt, out):
@@ -34,28 +34,34 @@ def tile_list_flow_anomaly_residuals_kernel(tc, tab_words, tab_scales, offs, w1,
         keep = ctx.enter_context(tc.tile_pool(name="keep", bufs=1))
         psum = ctx.enter_context(tc.psum_pool(name="psum", bufs=1))
 
+        spot = {"top": 0}
+
+        def place(name, shape, dtype, over=None, at=0):
+            size = WIDTH[dtype]
+            for n in shape[1:]:
+                size = size * n
+            if over is None:
+                spot[name] = spot["top"]
+                spot["top"] = spot["top"] + (size + 63) // 64 * 64
+            else:
+                spot[name] = spot[over] + at
+            return keep.tile(shape, dtype, name=name, align_bytes=64, offset=spot[name])
+
         offsets = lists.tile([P, S // 16], U16, name="offsets")
-        words = [keep.tile([P, T], I32, name=f"words{a}", align_bytes=64) for a in range(KA)]
-        tscale = keep.tile([P, T // 4], I32, name="tscale", align_bytes=64)
-        vcodes = [keep.tile([P, S], I32, name=f"vcodes{a}", align_bytes=64) for a in range(KA)]
-        vscale = keep.tile([P, S], U8, name="vscale", align_bytes=64)
-        raw = [[keep.tile([P, PACK, KP], F32, name=f"raw{b}_{a}", align_bytes=64) for a in range(KA)] for b in range(HB)]
-        wbf = {}
-        wcodes = [[keep.tile([P, KP], U32, name=f"wcodes{b}_{a}", align_bytes=64) for a in range(KA)] for b in range(HB)]
-        wscale = [[keep.tile([P, KP], U8, name=f"wscale{b}_{a}", align_bytes=64) for a in range(KA)] for b in range(HB)]
-        bias = keep.tile([P, HB, PACK], F32, name="bias")
-        weight = keep.tile([P, NC], F32, name="weight")
-        w4c = keep.tile([P, HB, 2 * N], U8, name="w4c", align_bytes=64)
-        w4s = keep.tile([P, HB, N // 4], I32, name="w4s", align_bytes=64)
-        gwin = [keep.tile([P, T], F32, name=f"gwin{c}", tag=f"gwin{c}", align_bytes=64) for c in range(NC)]
-        gpick0 = [keep.tile([P, TOK], F32, name=f"gpick0_{s}", tag=f"gpick0_{s}", align_bytes=64) for s in range(SH)]
-        gpick = [None] + [keep.tile([P, S], F32, name=f"gpick{c}", align_bytes=64) for c in range(1, NC)]
-        hrow = [[keep.tile([P, PACK, TOK], BF16, name=f"hrow{b}_{s}", align_bytes=64) for s in range(SH)] for b in range(HB)]
-        hint = [keep.tile([P, PACK * S], BF16, name=f"hint{b}", align_bytes=64) for b in range(HB)]
-        hcodes = {}
-        hscale = [keep.tile([P, S], U8, name=f"hscale{b}", align_bytes=64) for b in range(HB)]
-        diff = {}
-        diff_home = {0: "gwin3", 1: "diff1"}
+        words = [place(f"words{a}", [P, T], I32) for a in range(KA)]
+        tscale = place("tscale", [P, T // 4], I32)
+        vscale = place("vscale", [P, S], U8)
+        raw = [[place(f"raw{b}_{a}", [P, PACK, KP], F32) for a in range(KA)] for b in range(HB)]
+        wscale = [[place(f"wscale{b}_{a}", [P, KP], U8) for a in range(KA)] for b in range(HB)]
+        bias = place("bias", [P, HB, PACK], F32)
+        weight = place("weight", [P, NC], F32)
+        w4c = place("w4c", [P, HB, 2 * N], U8)
+        w4s = place("w4s", [P, HB, N // 4], I32)
+        gwin = [place(f"gwin{c}", [P, T], F32) for c in range(NC)]
+        hscale = [place(f"hscale{b}", [P, S], U8) for b in range(HB)]
+        hrow = [[place(f"hrow{b}_{s}", [P, PACK, TOK], BF16) for s in range(SH)] for b in range(HB)]
+        hint = {}
+        vcodes, wbf, wcodes, hcodes, gpick, diff = {}, {}, {}, {}, {}, {}
         banks = [[psum.tile([P, TOK], F32, name=f"bank{s}_{t}") for t in range(PACK)] for s in range(SH)]
 
         def offs_of(j0, j1):
@@ -68,13 +74,12 @@ def tile_list_flow_anomaly_residuals_kernel(tc, tab_words, tab_scales, offs, w1,
         def load_words(a):
             nc.sync.dma_start(out=words[a][:], in_=tab_words[a].rearrange("p t i -> p (t i)").bitcast(I32))
 
-        def load_tscale(first, last):
-            for a, r in [divmod(i, 4) for i in range(first, last)]:
-                nc.sync.dma_start(out=tscale[4 * a + r : P : 32, :], in_=tab_scales[a, r:16:4, :].bitcast(I32))
+        def load_g(c):
+            nc.sync.dma_start(out=gwin[c][:], in_=gT[c * P : (c + 1) * P, :])
 
-        def cast_w1(b, a, m0, m1, eng):
-            if m0 == 0:
-                wbf[b, a] = keep.tile([P, PACK * KP], BF16, name=f"wbf{b}_{a}", tag=f"wbf{a}", align_bytes=64)
+        def cast_w1(b, a, m0, m1, eng, over=None, at=0):
+            if (b, a) not in wbf:
+                wbf[b, a] = place(f"wbf{b}_{a}", [P, PACK * KP], BF16, over, at)
             dst = wbf[b, a][:].rearrange("p (t m j) -> p m j t", t=PACK, j=PACK)[:, m0:m1]
             src = raw[b][a][:].rearrange("p j (m t) -> p m j t", t=PACK)[:, m0:m1]
             if eng == "V":
@@ -82,43 +87,70 @@ def tile_list_flow_anomaly_residuals_kernel(tc, tab_words, tab_scales, offs, w1,
             else:
                 nc.scalar.copy(out=dst, in_=src)
 
-        def quant_w1(b, a):
-            nc.vector.quantize_mx(out=wcodes[b][a][:].bitcast(FP8X4), scales=wscale[b][a][:], in_=wbf[b, a][:])
+        def quant_w1(b, a, over=None, at=0):
+            wcodes[b, a] = place(f"wcodes{b}_{a}", [P, KP], U32, over, at)
+            nc.vector.quantize_mx(out=wcodes[b, a][:].bitcast(FP8X4), scales=wscale[b][a][:], in_=wbf[b, a][:])
 
-        def gather_words(a, j0, j1):
+        def cast_half(b, a, u, eng, over=None, at=0):
+            if (b, a) not in wbf:
+                wbf[b, a] = place(f"wbf{b}_{a}", [P, PACK * KP], BF16, over, at)
+            dst = wbf[b, a][:].rearrange("p (t m j) -> p m j t", t=PACK, j=PACK)[:, :, :, 2 * u : 2 * u + 2]
+            src = raw[b][a][:].rearrange("p j (m t) -> p m j t", t=PACK)[:, :, :, 2 * u : 2 * u + 2]
+            if eng == "V":
+                nc.vector.tensor_copy(out=dst, in_=src)
+            else:
+                nc.scalar.copy(out=dst, in_=src)
+
+        def quant_half(b, a, u, over=None, at=0):
+            if (b, a) not in wcodes:
+                wcodes[b, a] = place(f"wcodes{b}_{a}", [P, KP], U32, over, at)
+            cols = slice(u * KP // 2, (u + 1) * KP // 2)
+            nc.vector.quantize_mx(out=wcodes[b, a][:, cols].bitcast(FP8X4), scales=wscale[b][a][:, cols], in_=wbf[b, a][:, u * 2 * KP : (u + 1) * 2 * KP])
+
+        def gather_words(a, j0, j1, over=None, at=0):
+            if a not in vcodes:
+                vcodes[a] = place(f"vcodes{a}", [P, S], I32, over, at)
             nc.vector.tensor_copy(vcodes[a][:, j0:j1].bitcast(U32), words[a][:].bitcast(U32).indirect(offs_of(j0, j1)))
 
         def gather_scales():
             nc.vector.tensor_copy(vscale[:], tscale[:].bitcast(U8).indirect(offs_of(0, S)))
 
-        def mm1(b, a, s):
+        def mm1(b, a, s, first=0, last=KA - 1):
             for t in range(PACK):
                 cols = slice(t * P, (t + 1) * P)
                 nc.tensor.matmul_mx(
                     out=banks[s][t][:],
-                    lhsT=wcodes[b][a][:, cols].bitcast(FP8X4),
+                    lhsT=wcodes[b, a][:, cols].bitcast(FP8X4),
                     lhsT_scale=wscale[b][a][:, cols],
                     rhs=vcodes[a][:, s * TOK : (s + 1) * TOK].bitcast(FP8X4),
                     rhs_scale=vscale[PACK * a : P, s * TOK : (s + 1) * TOK],
-                    start=(a == 0),
-                    stop=(a == KA - 1),
+                    start=(a == first),
+                    stop=(a == last),
                 )
 
         def evac_h(b, s):
             for t in range(PACK):
                 nc.scalar.activation(out=hrow[b][s][:, t, :], in_=banks[s][t][:], func=ACT.Relu, bias=bias[:, b, t : t + 1])
 
+        def woven(b, j0, j1):
+            tile = place(f"hint{b}_{j0}", [P, PACK * (j1 - j0)], BF16)
+            for j in range(j0, j1, TOK):
+                hint[b, j // TOK] = tile[:, PACK * (j - j0) : PACK * (j - j0 + TOK)]
+            hint[b, j0, j1] = tile[:]
+
         def weave_h(b, s, c0, c1, eng):
-            dst = hint[b][:, s * PACK * TOK : (s + 1) * PACK * TOK].rearrange("p (c i t) -> p c t i", i=4, t=PACK)[:, c0:c1]
+            dst = hint[b, s].rearrange("p (c i t) -> p c t i", i=4, t=PACK)[:, c0:c1]
             src = hrow[b][s][:].rearrange("p t (c i) -> p c t i", i=4)[:, c0:c1]
             if eng == "V":
                 nc.vector.tensor_copy(out=dst, in_=src)
+            elif eng == "G":
+                nc.gpsimd.tensor_scalar(out=dst, in0=src, scalar1=1.0, scalar2=0.0, op0=ALU.mult, op1=ALU.add)
             else:
                 nc.scalar.copy(out=dst, in_=src)
 
-        def quant_h(b, j0, j1, home):
-            codes = keep.tile([P, j1 - j0], U32, name=f"hcodes{b}_{j0}", tag=home, align_bytes=64)
-            nc.vector.quantize_mx(out=codes[:].bitcast(FP8X4), scales=hscale[b][:, j0:j1], in_=hint[b][:, PACK * j0 : PACK * j1])
+        def quant_h(b, j0, j1, over=None, at=0):
+            codes = place(f"hcodes{b}_{j0}", [P, j1 - j0], U32, over, at)
+            nc.vector.quantize_mx(out=codes[:].bitcast(FP8X4), scales=hscale[b][:, j0:j1], in_=hint[b, j0, j1])
             for j in range(j0, j1, TOK):
                 hcodes[b, j // TOK] = codes[:, j - j0 : j - j0 + TOK]
 
@@ -134,106 +166,126 @@ def tile_list_flow_anomaly_residuals_kernel(tc, tab_words, tab_scales, offs, w1,
                     stop=(b == HB - 1),
                 )
 
-        def picked(c, j0, j1):
-            if c == 0:
-                return gpick0[j0 // TOK][:, j0 % TOK : j0 % TOK + j1 - j0]
-            return gpick[c][:, j0:j1]
+        def gather_g(c, j0, j1, over=None, at=0):
+            picked = place(f"gpick{c}_{j0}", [P, j1 - j0], F32, over, at)
+            nc.vector.tensor_copy(picked[:], gwin[c][:].indirect(offs_of(j0, j1)))
+            for j in range(j0, j1, TOK):
+                gpick[c, j // TOK] = picked[:, j - j0 : j - j0 + TOK]
 
-        def gather_g(c, j0, j1):
-            nc.vector.tensor_copy(picked(c, j0, j1), gwin[c][:].indirect(offs_of(j0, j1)))
-
-        def finish(c, s, j0, j1):
-            if s not in diff:
-                diff[s] = keep.tile([P, NC, TOK], F32, name=f"diff{s}", tag=diff_home[s], align_bytes=64)
-            d = diff[s][:, c, j0:j1]
-            nc.vector.tensor_tensor(out=d, in0=banks[s][c][:, j0:j1], in1=picked(c, s * TOK + j0, s * TOK + j1), op=ALU.subtract)
+        def finish(c, s, j0, j1, over=None, at=0):
+            if (c, s) not in diff:
+                diff[c, s] = place(f"diff{c}_{s}", [P, TOK], F32, over, at)
+            d = diff[c, s][:, j0:j1]
+            nc.vector.tensor_tensor(out=d, in0=banks[s][c][:, j0:j1], in1=gpick[c, s][:, j0:j1], op=ALU.subtract)
             nc.scalar.activation(out=d, in_=d, func=ACT.Abs, scale=weight[:, c : c + 1])
             nc.sync.dma_start(out=out[c * P : (c + 1) * P, s * TOK + j0 : s * TOK + j1], in_=d)
+
+        def load_bias(queue):
+            queue.dma_start(out=bias[:], in_=b1.rearrange("(b p t) -> p b t", b=HB, t=PACK))
+
+        def load_weight(queue):
+            with nc.allow_non_contiguous_dma(reason="one weight a partition"):
+                queue.dma_start(out=weight[:], in_=wgt.rearrange("(c p) -> p c", p=P))
+
+        def load_w4_codes():
+            nc.sync.dma_start(out=w4c[:].bitcast(I32), in_=w4_words.rearrange("a p n -> p a n").bitcast(I32))
+
+        def load_w4_scales(queue):
+            for r in range(4):
+                queue.dma_start(out=w4s[r:P:32, :, :], in_=w4_scales[:, r:16:4, :].rearrange("a q n -> q a n").bitcast(I32))
+
+        def load_tscale_quadrants(queue):
+            for q in range(4):
+                queue.dma_start(out=tscale[32 * q : 32 * q + 4 * KA, :], in_=tab_scales[:, 4 * q : 4 * q + 4, :].bitcast(I32))
+
+        def load_tscale(first, last):
+            for r, a in [divmod(i, KA) for i in range(first, last)]:
+                nc.sync.dma_start(out=tscale[4 * a + r : P : 32, :], in_=tab_scales[a, r:16:4, :].bitcast(I32))
 
         nc.sync.dma_start(offsets[:], offs)
         nc.gpsimd.memset(tscale[:], 0)
         nc.gpsimd.memset(w4s[:], 0)
         load_words(0)
         load_tscale(0, 6)
-        load_words(1)
-        load_tscale(6, 12)
         load_w1(0, 0)
-        nc.sync.dma_start(out=bias[:], in_=b1.rearrange("(b p t) -> p b t", b=HB, t=PACK))
+        load_tscale(6, 12)
+        load_words(1)
         load_w1(0, 1)
-        load_w1(0, 2)
         load_words(2)
+        load_w1(0, 2)
+        load_bias(nc.sync)
         load_w1(1, 0)
         load_w1(1, 1)
         load_w1(1, 2)
-        nc.sync.dma_start(out=gwin[0][:], in_=gT[0 * P : (0 + 1) * P, :])
-        nc.sync.dma_start(out=gwin[1][:], in_=gT[1 * P : (1 + 1) * P, :])
-        nc.sync.dma_start(out=gwin[2][:], in_=gT[2 * P : (2 + 1) * P, :])
-        nc.sync.dma_start(out=w4c[:].bitcast(I32), in_=w4_words.rearrange("a p n -> p a n").bitcast(I32))
-        for r in range(4):
-            nc.sync.dma_start(
-                out=w4s[r:P:32, :, :],
-                in_=w4_scales[:, r:16:4, :].rearrange("a q n -> q a n").bitcast(I32),
-            )
-        nc.sync.dma_start(out=gwin[3][:], in_=gT[3 * P : (3 + 1) * P, :])
-        with nc.allow_non_contiguous_dma(reason="one weight a partition"):
-            nc.sync.dma_start(out=weight[:], in_=wgt.rearrange("(c p) -> p c", p=P))
+        load_g(0)
+        load_g(1)
+        load_g(2)
+        load_w4_codes()
+        load_w4_scales(nc.sync)
+        load_g(3)
+        load_weight(nc.sync)
         gather_words(0, 0, S)
-        gather_words(1, 0, S)
-        cast_w1(0, 0, 0, 128, "S")
         gather_scales()
+        cast_w1(0, 0, 0, 128, "S")
         quant_w1(0, 0)
         mm1(0, 0, 0)
         mm1(0, 0, 1)
-        cast_w1(0, 1, 0, 64, "S")
-        cast_w1(0, 1, 64, 128, "V")
+        gather_words(1, 0, S)
+        cast_w1(0, 1, 0, 56, "S")
+        cast_w1(0, 1, 56, 128, "V")
         quant_w1(0, 1)
         mm1(0, 1, 0)
         mm1(0, 1, 1)
-        cast_w1(0, 2, 0, 64, "S")
-        cast_w1(0, 2, 64, 128, "V")
-        quant_w1(0, 2)
-        gather_words(2, 0, TOK)
+        gather_words(2, 0, S)
+        cast_half(0, 2, 0, "V")
+        cast_half(0, 2, 1, "S")
+        quant_half(0, 2, 0, "words0", 0)
+        quant_half(0, 2, 1)
         mm1(0, 2, 0)
-        gather_words(2, TOK, S)
         mm1(0, 2, 1)
+        for b in range(HB):
+            for s in range(SH):
+                woven(b, s * TOK, (s + 1) * TOK)
         evac_h(0, 0)
-        evac_h(0, 1)
-        cast_w1(1, 0, 0, 128, "V")
-        quant_w1(1, 0)
-        mm1(1, 0, 0)
-        mm1(1, 0, 1)
-        cast_w1(1, 1, 0, 128, "V")
-        quant_w1(1, 1)
-        mm1(1, 1, 0)
-        cast_w1(1, 2, 0, 128, "V")
-        quant_w1(1, 2)
-        mm1(1, 2, 0)
-        mm1(1, 1, 1)
-        mm1(1, 2, 1)
         weave_h(0, 0, 0, 128, "S")
+        evac_h(0, 1)
         weave_h(0, 1, 0, 128, "S")
-        gather_g(0, 0, TOK)
-        gather_g(0, TOK, S)
-        gather_g(1, 0, S)
-        quant_h(0, 0, S, "gwin1")
+        cast_w1(1, 0, 0, 128, "V", "wbf0_0")
+        quant_w1(1, 0, "words0", 2048)
+        mm1(1, 0, 0)
+        cast_w1(1, 1, 0, 128, "V", "wbf0_1")
+        quant_w1(1, 1, "words0", 4096)
+        mm1(1, 1, 0)
+        cast_half(1, 2, 0, "V", "wbf0_2")
+        cast_half(1, 2, 1, "V")
+        quant_half(1, 2, 0, "words0", 6144)
+        quant_half(1, 2, 1)
+        quant_h(0, 0, TOK, "raw1_2")
+        mm1(1, 2, 0)
+        mm1(1, 2, 1, 2, 1)
+        mm1(1, 0, 1, 2, 1)
+        mm1(1, 1, 1, 2, 1)
+        gather_g(0, 0, S, "raw0_0", 0)
+        gather_g(1, 0, S, "raw0_0", 4096)
         evac_h(1, 0)
         mm2(0, 0)
         weave_h(1, 0, 0, 128, "S")
         evac_h(1, 1)
-        mm2(0, 1)
         weave_h(1, 1, 0, 128, "S")
-        gather_g(2, 0, S)
-        quant_h(1, 0, TOK, "gwin2")
+        gather_g(2, 0, S, "raw0_1", 0)
+        quant_h(1, 0, TOK, "gwin2", 0)
+        quant_h(0, TOK, S, "gwin2", 2048)
         mm2(1, 0)
-        gather_g(3, 0, S)
-        finish(0, 0, 0, TOK)
-        quant_h(1, TOK, S, "gpick0_0")
+        mm2(0, 1)
+        finish(0, 0, 0, TOK, "raw1_0", 0)
+        finish(1, 0, 0, TOK, "raw1_0", 2048)
+        gather_g(3, 0, S, "raw0_1", 4096)
+        quant_h(1, TOK, S, "gwin3", 0)
         mm2(1, 1)
-        finish(1, 0, 0, TOK)
-        finish(2, 0, 0, TOK)
-        finish(3, 0, 0, TOK)
-        finish(0, 1, 0, TOK)
-        finish(1, 1, 0, TOK)
-        finish(2, 1, 0, TOK)
-        finish(3, 1, 0, 384)
+        finish(2, 0, 0, TOK, "gwin3", 2048)
+        finish(3, 0, 0, TOK, "raw1_0", 6144)
+        finish(0, 1, 0, TOK, "raw0_2", 0)
+        finish(1, 1, 0, TOK, "raw0_2", 2048)
+        finish(2, 1, 0, TOK, "raw0_2", 4096)
+        finish(3, 1, 0, 384, "raw0_2", 6144)
         finish(3, 1, 384, TOK)

@@ -61,7 +61,7 @@ def tile_list_flow_anomaly_residuals_kernel(tc, tab_words, tab_scales, offs, w1,
         hscale = [place(f"hscale{b}", [P, S], U8) for b in range(HB)]
         hrow = [[place(f"hrow{b}_{s}", [P, PACK, TOK], BF16) for s in range(SH)] for b in range(HB)]
         hint = {}
-        vcodes, wbf, wcodes, hcodes, gpick, diff = {}, {}, {}, {}, {}, {}
+        vcodes, wbf, wcodes, hcodes, gpick, diff, ysb = {}, {}, {}, {}, {}, {}, {}
         banks = [[psum.tile([P, TOK], F32, name=f"bank{s}_{t}") for t in range(PACK)] for s in range(SH)]
 
         def offs_of(j0, j1):
@@ -128,12 +128,17 @@ def tile_list_flow_anomaly_residuals_kernel(tc, tab_words, tab_scales, offs, w1,
                     stop=(a == last),
                 )
 
-        def evac_h(b, s):
+        def evac_h(b, s, on_vector=()):
             for t in range(PACK):
-                nc.scalar.activation(out=hrow[b][s][:, t, :], in_=banks[s][t][:], func=ACT.Relu, bias=bias[:, b, t : t + 1])
+                if t in on_vector:
+                    nc.vector.tensor_scalar(
+                        out=hrow[b][s][:, t, :], in0=banks[s][t][:], scalar1=bias[:, b, t : t + 1], scalar2=0.0, op0=ALU.add, op1=ALU.max
+                    )
+                else:
+                    nc.scalar.activation(out=hrow[b][s][:, t, :], in_=banks[s][t][:], func=ACT.Relu, bias=bias[:, b, t : t + 1])
 
-        def woven(b, j0, j1):
-            tile = place(f"hint{b}_{j0}", [P, PACK * (j1 - j0)], BF16)
+        def woven(b, j0, j1, over=None, at=0):
+            tile = place(f"hint{b}_{j0}", [P, PACK * (j1 - j0)], BF16, over, at)
             for j in range(j0, j1, TOK):
                 hint[b, j // TOK] = tile[:, PACK * (j - j0) : PACK * (j - j0 + TOK)]
             hint[b, j0, j1] = tile[:]
@@ -154,8 +159,8 @@ def tile_list_flow_anomaly_residuals_kernel(tc, tab_words, tab_scales, offs, w1,
             for j in range(j0, j1, TOK):
                 hcodes[b, j // TOK] = codes[:, j - j0 : j - j0 + TOK]
 
-        def mm2(b, s):
-            for c in range(NC):
+        def mm2(b, s, order=(0, 1, 2, 3)):
+            for c in order:
                 nc.tensor.matmul_mx(
                     out=banks[s][c][:],
                     lhsT=w4c[:, b, 2 * c * P : 2 * (c + 1) * P].bitcast(FP4X4),
@@ -179,6 +184,16 @@ def tile_list_flow_anomaly_residuals_kernel(tc, tab_words, tab_scales, offs, w1,
             nc.vector.tensor_tensor(out=d, in0=banks[s][c][:, j0:j1], in1=gpick[c, s][:, j0:j1], op=ALU.subtract)
             nc.scalar.activation(out=d, in_=d, func=ACT.Abs, scale=weight[:, c : c + 1])
             nc.sync.dma_start(out=out[c * P : (c + 1) * P, s * TOK + j0 : s * TOK + j1], in_=d)
+
+        def copy_y(c, s, over=None, at=0):
+            ysb[c, s] = place(f"y{c}_{s}", [P, TOK], F32, over, at)
+            nc.scalar.copy(out=ysb[c, s][:], in_=banks[s][c][:])
+
+        def finish_fused(c, s, over=None, at=0):
+            d = place(f"diff{c}_{s}", [P, TOK], F32, over, at)
+            nc.vector.tensor_tensor(out=d[:], in0=gwin[c][:].indirect(offs_of(s * TOK, (s + 1) * TOK)), in1=ysb[c, s][:], op=ALU.subtract)
+            nc.scalar.activation(out=d[:], in_=d[:], func=ACT.Abs, scale=weight[:, c : c + 1])
+            nc.sync.dma_start(out=out[c * P : (c + 1) * P, s * TOK : (s + 1) * TOK], in_=d[:])
 
         def load_bias(queue):
             queue.dma_start(out=bias[:], in_=b1.rearrange("(b p t) -> p b t", b=HB, t=PACK))
@@ -243,9 +258,9 @@ def tile_list_flow_anomaly_residuals_kernel(tc, tab_words, tab_scales, offs, w1,
         quant_half(0, 2, 1)
         mm1(0, 2, 0)
         mm1(0, 2, 1)
-        for b in range(HB):
-            for s in range(SH):
-                woven(b, s * TOK, (s + 1) * TOK)
+        woven(0, 0, TOK)
+        woven(0, TOK, S)
+        woven(1, 0, TOK)
         evac_h(0, 0)
         weave_h(0, 0, 0, 128, "S")
         evac_h(0, 1)
@@ -265,25 +280,28 @@ def tile_list_flow_anomaly_residuals_kernel(tc, tab_words, tab_scales, offs, w1,
         mm1(1, 2, 1, 2, 1)
         mm1(1, 0, 1, 2, 1)
         mm1(1, 1, 1, 2, 1)
-        gather_g(0, 0, S, "raw0_0", 0)
+        gather_g(0, 0, TOK, "raw1_1", 2048)
+        gather_g(0, TOK, S, "raw0_0", 0)
         gather_g(1, 0, S, "raw0_0", 4096)
         evac_h(1, 0)
         mm2(0, 0)
         weave_h(1, 0, 0, 128, "S")
         evac_h(1, 1)
-        weave_h(1, 1, 0, 128, "S")
         gather_g(2, 0, S, "raw0_1", 0)
         quant_h(1, 0, TOK, "gwin2", 0)
         quant_h(0, TOK, S, "gwin2", 2048)
-        mm2(1, 0)
+        mm2(1, 0, (0, 3, 1, 2))
+        copy_y(3, 0, "raw1_1", 0)
         mm2(0, 1)
         finish(0, 0, 0, TOK, "raw1_0", 0)
-        finish(1, 0, 0, TOK, "raw1_0", 2048)
-        gather_g(3, 0, S, "raw0_1", 4096)
+        woven(1, TOK, S, "gpick0_0")
+        weave_h(1, 1, 0, 128, "S")
+        gather_g(3, TOK, S, "raw0_1", 4096)
+        finish_fused(3, 0, "raw1_0", 6144)
+        finish(1, 0, 0, TOK, "gwin3", 4096)
         quant_h(1, TOK, S, "gwin3", 0)
         mm2(1, 1)
-        finish(2, 0, 0, TOK, "gwin3", 2048)
-        finish(3, 0, 0, TOK, "raw1_0", 6144)
+        finish(2, 0, 0, TOK, "hint1_512")
         finish(0, 1, 0, TOK, "raw0_2", 0)
         finish(1, 1, 0, TOK, "raw0_2", 2048)
         finish(2, 1, 0, TOK, "raw0_2", 4096)

@@ -149,6 +149,8 @@ def tile_list_flow_anomaly_residuals_kernel(tc, tab_words, tab_scales, offs, w1,
             if eng == "V":
                 nc.vector.tensor_copy(out=dst, in_=src)
             elif eng == "G":
+                dst = hint[b, s].rearrange("p (j t) -> p j t", t=PACK)[:, 4 * c0 : 4 * c1]
+                src = hrow[b][s][:].rearrange("p t j -> p j t")[:, 4 * c0 : 4 * c1]
                 nc.gpsimd.tensor_scalar(out=dst, in0=src, scalar1=1.0, scalar2=0.0, op0=ALU.mult, op1=ALU.add)
             else:
                 nc.scalar.copy(out=dst, in_=src)
@@ -285,7 +287,7 @@ def tile_list_flow_anomaly_residuals_kernel(tc, tab_words, tab_scales, offs, w1,
         gather_g(1, 0, S, "raw0_0", 4096)
         evac_h(1, 0)
         mm2(0, 0)
-        weave_h(1, 0, 0, 128, "S")
+        weave_h(1, 0, 0, 128, "G")
         evac_h(1, 1)
         gather_g(2, 0, S, "raw0_1", 0)
         quant_h(1, 0, TOK, "gwin2", 0)

@@ -161,6 +161,35 @@ def tile_list_flow_anomaly_residuals_kernel(tc, tab_words, tab_scales, offs, w1,
             for j in range(j0, j1, TOK):
                 hcodes[b, j // TOK] = codes[:, j - j0 : j - j0 + TOK]
 
+        def mm1_banks(b, s, passes, first, last):
+            for t in range(PACK):
+                cols = slice(t * P, (t + 1) * P)
+                for a in passes:
+                    nc.tensor.matmul_mx(
+                        out=banks[s][t][:],
+                        lhsT=wcodes[b, a][:, cols].bitcast(FP8X4),
+                        lhsT_scale=wscale[b][a][:, cols],
+                        rhs=vcodes[a][:, s * TOK : (s + 1) * TOK].bitcast(FP8X4),
+                        rhs_scale=vscale[PACK * a : P, s * TOK : (s + 1) * TOK],
+                        start=(a == first),
+                        stop=(a == last),
+                    )
+
+        def weave_part(b, s, tile, j0, j1, at, eng):
+            src = hrow[b][s][:, :, j0:j1]
+            dst = tile[:, PACK * at : PACK * (at + j1 - j0)]
+            if eng == "G":
+                nc.gpsimd.tensor_scalar(
+                    out=dst.rearrange("p (j t) -> p j t", t=PACK), in0=src.rearrange("p t j -> p j t"), scalar1=1.0, scalar2=0.0, op0=ALU.mult, op1=ALU.add
+                )
+            else:
+                nc.scalar.copy(out=dst.rearrange("p (c i t) -> p c t i", i=4, t=PACK), in_=src.rearrange("p t (c i) -> p c t i", i=4))
+
+        def quant_part(b, s, tile, j0, j1, over=None, at=0):
+            if (b, s) not in hcodes:
+                hcodes[b, s] = place(f"hcodes{b}_{s}", [P, TOK], U32, over, at)[:]
+            nc.vector.quantize_mx(out=hcodes[b, s][:, j0:j1].bitcast(FP8X4), scales=hscale[b][:, s * TOK + j0 : s * TOK + j1], in_=tile[:])
+
         def mm2(b, s, order=(0, 1, 2, 3)):
             for c in order:
                 nc.tensor.matmul_mx(
@@ -191,11 +220,13 @@ def tile_list_flow_anomaly_residuals_kernel(tc, tab_words, tab_scales, offs, w1,
             ysb[c, s] = place(f"y{c}_{s}", [P, TOK], F32, over, at)
             nc.scalar.copy(out=ysb[c, s][:], in_=banks[s][c][:])
 
-        def finish_fused(c, s, over=None, at=0):
-            d = place(f"diff{c}_{s}", [P, TOK], F32, over, at)
-            nc.vector.tensor_tensor(out=d[:], in0=gwin[c][:].indirect(offs_of(s * TOK, (s + 1) * TOK)), in1=ysb[c, s][:], op=ALU.subtract)
-            nc.scalar.activation(out=d[:], in_=d[:], func=ACT.Abs, scale=weight[:, c : c + 1])
-            nc.sync.dma_start(out=out[c * P : (c + 1) * P, s * TOK : (s + 1) * TOK], in_=d[:])
+        def finish_fused(c, s, j0, j1, over=None, at=0):
+            if (c, s) not in diff:
+                diff[c, s] = place(f"diff{c}_{s}", [P, TOK], F32, over, at)
+            d = diff[c, s][:, j0:j1]
+            nc.vector.tensor_tensor(out=d, in0=gwin[c][:].indirect(offs_of(s * TOK + j0, s * TOK + j1)), in1=ysb[c, s][:, j0:j1], op=ALU.subtract)
+            nc.scalar.activation(out=d, in_=d, func=ACT.Abs, scale=weight[:, c : c + 1])
+            nc.sync.dma_start(out=out[c * P : (c + 1) * P, s * TOK + j0 : s * TOK + j1], in_=d)
 
         def load_bias(queue):
             queue.dma_start(out=bias[:], in_=b1.rearrange("(b p t) -> p b t", b=HB, t=PACK))
@@ -236,11 +267,11 @@ def tile_list_flow_anomaly_residuals_kernel(tc, tab_words, tab_scales, offs, w1,
         load_w1(1, 2)
         load_g(0)
         load_g(1)
-        load_g(2)
         load_w4_codes()
         load_w4_scales(nc.sync)
-        load_g(3)
         load_weight(nc.sync)
+        load_g(2)
+        load_g(3)
         gather_words(0, 0, S)
         gather_scales()
         cast_w1(0, 0, 0, 128, "S")
@@ -260,52 +291,57 @@ def tile_list_flow_anomaly_residuals_kernel(tc, tab_words, tab_scales, offs, w1,
         quant_half(0, 2, 1)
         mm1(0, 2, 0)
         mm1(0, 2, 1)
-        woven(0, 0, TOK)
-        woven(0, TOK, S)
-        woven(1, 0, TOK)
-        evac_h(0, 0)
-        weave_h(0, 0, 0, 128, "S")
+        HALF = TOK // 2
+        evac_h(0, 0, (1,))
+        hint00 = place("hint00", [P, PACK * TOK], BF16)
+        weave_part(0, 0, hint00, 0, TOK, 0, "S")
         evac_h(0, 1)
-        weave_h(0, 1, 0, 128, "S")
+        hint01a = place("hint01a", [P, PACK * HALF], BF16)
+        weave_part(0, 1, hint01a, 0, HALF, 0, "S")
         cast_w1(1, 0, 0, 128, "V", "wbf0_0")
         quant_w1(1, 0, "words0", 2048)
         mm1(1, 0, 0)
         cast_w1(1, 1, 0, 128, "V", "wbf0_1")
+        quant_part(0, 0, hint00, 0, TOK, "raw1_1")
         quant_w1(1, 1, "words0", 4096)
+        mm1(1, 0, 1, 0, 1)
         mm1(1, 1, 0)
         cast_half(1, 2, 0, "V", "wbf0_2")
         cast_half(1, 2, 1, "V")
         quant_half(1, 2, 0, "words0", 6144)
         quant_half(1, 2, 1)
-        quant_h(0, 0, TOK, "raw1_2")
         mm1(1, 2, 0)
-        mm1(1, 2, 1, 2, 1)
-        mm1(1, 0, 1, 2, 1)
-        mm1(1, 1, 1, 2, 1)
-        gather_g(0, 0, TOK, "raw1_1", 2048)
-        gather_g(0, TOK, S, "raw0_0", 0)
-        gather_g(1, 0, S, "raw0_0", 4096)
+        mm1_banks(1, 1, (2, 1), 0, 1)
+        hint01b = place("hint01b", [P, PACK * HALF], BF16, "wbf1_2")
+        weave_part(0, 1, hint01b, HALF, TOK, 0, "G")
+        gather_g(0, 0, S, "raw0_0", 0)
+        quant_part(0, 1, hint01a, 0, HALF, "gwin0")
+        quant_part(0, 1, hint01b, HALF, TOK)
         evac_h(1, 0)
+        hint10 = place("hint10", [P, PACK * TOK], BF16, "wbf1_2")
+        weave_part(1, 0, hint10, 0, 96, 0, "S")
+        weave_part(1, 0, hint10, 96, TOK, 96, "G")
         mm2(0, 0)
-        weave_h(1, 0, 0, 128, "G")
         evac_h(1, 1)
-        gather_g(2, 0, S, "raw0_1", 0)
-        quant_h(1, 0, TOK, "gwin2", 0)
-        quant_h(0, TOK, S, "gwin2", 2048)
-        mm2(1, 0, (0, 3, 1, 2))
-        copy_y(3, 0, "raw1_1", 0)
         mm2(0, 1)
-        finish(0, 0, 0, TOK, "raw1_0", 0)
-        woven(1, TOK, S, "gpick0_0")
-        weave_h(1, 1, 0, 128, "S")
-        gather_g(3, TOK, S, "raw0_1", 4096)
-        finish_fused(3, 0, "raw1_0", 6144)
-        finish(1, 0, 0, TOK, "gwin3", 4096)
-        quant_h(1, TOK, S, "gwin3", 0)
-        mm2(1, 1)
-        finish(2, 0, 0, TOK, "hint1_512")
+        gather_g(1, 0, S, "raw0_0", 4096)
+        quant_part(1, 0, hint10, 0, TOK, "gwin1")
+        hint11 = place("hint11", [P, PACK * TOK], BF16, "wbf1_2")
+        weave_part(1, 1, hint11, 0, 304, 0, "S")
+        weave_part(1, 1, hint11, 304, TOK, 304, "G")
+        mm2(1, 0, (2, 0, 1, 3))
+        gather_g(2, 0, TOK, "raw0_1", 0)
+        finish(2, 0, 0, TOK, "raw1_0", 0)
+        quant_part(1, 1, hint11, 0, TOK, "gpick2_0")
+        copy_y(3, 0, "raw1_2", 0)
+        mm2(1, 1, (2, 0, 1, 3))
+        finish(0, 0, 0, TOK, "hint11", 0)
+        finish(1, 0, 0, TOK, "hint11", 2048)
+        copy_y(2, 1, "raw1_2", 2048)
+        finish_fused(3, 0, 0, TOK, "raw1_0", 2048)
+        copy_y(3, 1, "raw1_2", 4096)
         finish(0, 1, 0, TOK, "raw0_2", 0)
         finish(1, 1, 0, TOK, "raw0_2", 2048)
-        finish(2, 1, 0, TOK, "raw0_2", 4096)
-        finish(3, 1, 0, 384, "raw0_2", 6144)
-        finish(3, 1, 384, TOK)
+        finish_fused(2, 1, 0, TOK, "raw0_2", 4096)
+        finish_fused(3, 1, 0, 384, "raw0_2", 6144)
+        finish_fused(3, 1, 384, TOK)

@@ -213,8 +213,9 @@ def tile_list_flow_anomaly_residuals_kernel(tc, tab_words, tab_scales, offs, w1,
                 diff[c, s] = place(f"diff{c}_{s}", [P, TOK], F32, over, at)
             d = diff[c, s][:, j0:j1]
             nc.vector.tensor_tensor(out=d, in0=banks[s][c][:, j0:j1], in1=gpick[c, s][:, j0:j1], op=ALU.subtract)
-            nc.scalar.activation(out=d, in_=d, func=ACT.Abs, scale=weight[:, c : c + 1])
-            nc.sync.dma_start(out=out[c * P : (c + 1) * P, s * TOK + j0 : s * TOK + j1], in_=d)
+            res = place(f"res{c}_{s}", [P, j1 - j0], F32)
+            nc.scalar.activation(out=res[:], in_=d, func=ACT.Abs, scale=weight[:, c : c + 1])
+            nc.sync.dma_start(out=out[c * P : (c + 1) * P, s * TOK + j0 : s * TOK + j1], in_=res[:])
 
         def copy_y(c, s, over=None, at=0):
             ysb[c, s] = place(f"y{c}_{s}", [P, TOK], F32, over, at)
@@ -255,9 +256,9 @@ def tile_list_flow_anomaly_residuals_kernel(tc, tab_words, tab_scales, offs, w1,
         nc.gpsimd.memset(w4s[:], 0)
         load_words(0)
         load_tscale(0, 6)
-        load_w1(0, 0)
-        load_tscale(6, 12)
         load_words(1)
+        load_tscale(6, 12)
+        load_w1(0, 0)
         load_w1(0, 1)
         load_words(2)
         load_w1(0, 2)
@@ -273,38 +274,33 @@ def tile_list_flow_anomaly_residuals_kernel(tc, tab_words, tab_scales, offs, w1,
         load_g(2)
         load_g(3)
         gather_words(0, 0, S)
+        gather_words(1, 0, S)
         gather_scales()
         cast_w1(0, 0, 0, 128, "S")
         quant_w1(0, 0)
         mm1(0, 0, 0)
-        mm1(0, 0, 1)
-        gather_words(1, 0, S)
-        cast_w1(0, 1, 0, 56, "S")
-        cast_w1(0, 1, 56, 128, "V")
+        mm1(0, 0, 1, 0, 1)
+        cast_w1(0, 1, 0, 64, "S")
+        cast_w1(0, 1, 64, 128, "V")
         quant_w1(0, 1)
         mm1(0, 1, 0)
-        mm1(0, 1, 1)
         gather_words(2, 0, S)
         cast_half(0, 2, 0, "V")
         cast_half(0, 2, 1, "S")
         quant_half(0, 2, 0, "words0", 0)
         quant_half(0, 2, 1)
         mm1(0, 2, 0)
-        mm1(0, 2, 1)
-        HALF = TOK // 2
-        evac_h(0, 0, (1,))
+        mm1_banks(0, 1, (2, 1), 0, 1)
+        evac_h(0, 0)
+        evac_h(0, 1)
         hint00 = place("hint00", [P, PACK * TOK], BF16)
         weave_part(0, 0, hint00, 0, TOK, 0, "S")
-        evac_h(0, 1)
-        hint01a = place("hint01a", [P, PACK * HALF], BF16)
-        weave_part(0, 1, hint01a, 0, HALF, 0, "S")
         cast_w1(1, 0, 0, 128, "V", "wbf0_0")
         quant_w1(1, 0, "words0", 2048)
         mm1(1, 0, 0)
-        cast_w1(1, 1, 0, 128, "V", "wbf0_1")
-        quant_part(0, 0, hint00, 0, TOK, "raw1_1")
-        quant_w1(1, 1, "words0", 4096)
         mm1(1, 0, 1, 0, 1)
+        cast_w1(1, 1, 0, 128, "V", "wbf0_1")
+        quant_w1(1, 1, "words0", 4096)
         mm1(1, 1, 0)
         cast_half(1, 2, 0, "V", "wbf0_2")
         cast_half(1, 2, 1, "V")
@@ -312,36 +308,34 @@ def tile_list_flow_anomaly_residuals_kernel(tc, tab_words, tab_scales, offs, w1,
         quant_half(1, 2, 1)
         mm1(1, 2, 0)
         mm1_banks(1, 1, (2, 1), 0, 1)
-        hint01b = place("hint01b", [P, PACK * HALF], BF16, "wbf1_2")
-        weave_part(0, 1, hint01b, HALF, TOK, 0, "G")
+        hint01 = place("hint01", [P, PACK * TOK], BF16, "wbf1_2")
+        weave_part(0, 1, hint01, 0, TOK, 0, "G")
         gather_g(0, 0, S, "raw0_0", 0)
-        quant_part(0, 1, hint01a, 0, HALF, "gwin0")
-        quant_part(0, 1, hint01b, HALF, TOK)
+        quant_part(0, 0, hint00, 0, TOK, "gwin0")
+        quant_part(0, 1, hint01, 0, TOK, "gwin0", 2048)
         evac_h(1, 0)
         hint10 = place("hint10", [P, PACK * TOK], BF16, "wbf1_2")
-        weave_part(1, 0, hint10, 0, 96, 0, "S")
-        weave_part(1, 0, hint10, 96, TOK, 96, "G")
+        weave_part(1, 0, hint10, 0, TOK, 0, "G")
         mm2(0, 0)
         evac_h(1, 1)
         mm2(0, 1)
         gather_g(1, 0, S, "raw0_0", 4096)
         quant_part(1, 0, hint10, 0, TOK, "gwin1")
-        hint11 = place("hint11", [P, PACK * TOK], BF16, "wbf1_2")
-        weave_part(1, 1, hint11, 0, 304, 0, "S")
-        weave_part(1, 1, hint11, 304, TOK, 304, "G")
-        mm2(1, 0, (2, 0, 1, 3))
-        gather_g(2, 0, TOK, "raw0_1", 0)
-        finish(2, 0, 0, TOK, "raw1_0", 0)
-        quant_part(1, 1, hint11, 0, TOK, "gpick2_0")
-        copy_y(3, 0, "raw1_2", 0)
-        mm2(1, 1, (2, 0, 1, 3))
-        finish(0, 0, 0, TOK, "hint11", 0)
-        finish(1, 0, 0, TOK, "hint11", 2048)
-        copy_y(2, 1, "raw1_2", 2048)
-        finish_fused(3, 0, 0, TOK, "raw1_0", 2048)
-        copy_y(3, 1, "raw1_2", 4096)
-        finish(0, 1, 0, TOK, "raw0_2", 0)
-        finish(1, 1, 0, TOK, "raw0_2", 2048)
+        hint11 = place("hint11", [P, PACK * TOK], BF16)
+        weave_part(1, 1, hint11, 0, TOK, 0, "S")
+        mm2(1, 0)
+        quant_part(1, 1, hint11, 0, TOK, "gwin1", 2048)
+        mm2(1, 1)
+        copy_y(2, 0, "raw1_2", 0)
+        copy_y(3, 0, "raw1_2", 2048)
+        finish(0, 0, 0, TOK, "raw1_0", 0)
+        finish(1, 0, 0, TOK, "raw1_0", 2048)
+        copy_y(2, 1, "diff0_0")
+        copy_y(3, 1, "diff1_0")
+        finish_fused(2, 0, 0, TOK, "raw0_2", 0)
+        finish(0, 1, 0, TOK, "raw1_0", 4096)
+        finish_fused(3, 0, 0, TOK, "raw0_2", 2048)
+        finish(1, 1, 0, TOK, "raw1_0", 6144)
         finish_fused(2, 1, 0, TOK, "raw0_2", 4096)
         finish_fused(3, 1, 0, 384, "raw0_2", 6144)
         finish_fused(3, 1, 384, TOK)

@@ -92,9 +92,8 @@ def tile_list_flow_anomaly_residuals_kernel(tc, tab_words, tab_scales, offs, w1,
             nc.vector.quantize_mx(out=wcodes[b, a][:].bitcast(FP8X4), scales=wscale[b][a][:], in_=wbf[b, a][:])
 
         def cast_half(b, a, u, eng, over=None, at=0):
-            if (b, a) not in wbf:
-                wbf[b, a] = place(f"wbf{b}_{a}", [P, PACK * KP], BF16, over, at)
-            dst = wbf[b, a][:].rearrange("p (t m j) -> p m j t", t=PACK, j=PACK)[:, :, :, 2 * u : 2 * u + 2]
+            wbf[b, a, u] = place(f"wbf{b}_{a}_{u}", [P, 2 * KP], BF16, over, at)
+            dst = wbf[b, a, u][:].rearrange("p (t m j) -> p m j t", t=2, j=PACK)
             src = raw[b][a][:].rearrange("p j (m t) -> p m j t", t=PACK)[:, :, :, 2 * u : 2 * u + 2]
             if eng == "V":
                 nc.vector.tensor_copy(out=dst, in_=src)
@@ -105,7 +104,7 @@ def tile_list_flow_anomaly_residuals_kernel(tc, tab_words, tab_scales, offs, w1,
             if (b, a) not in wcodes:
                 wcodes[b, a] = place(f"wcodes{b}_{a}", [P, KP], U32, over, at)
             cols = slice(u * KP // 2, (u + 1) * KP // 2)
-            nc.vector.quantize_mx(out=wcodes[b, a][:, cols].bitcast(FP8X4), scales=wscale[b][a][:, cols], in_=wbf[b, a][:, u * 2 * KP : (u + 1) * 2 * KP])
+            nc.vector.quantize_mx(out=wcodes[b, a][:, cols].bitcast(FP8X4), scales=wscale[b][a][:, cols], in_=wbf[b, a, u][:])
 
         def gather_words(a, j0, j1, over=None, at=0):
             if a not in vcodes:
@@ -302,19 +301,20 @@ def tile_list_flow_anomaly_residuals_kernel(tc, tab_words, tab_scales, offs, w1,
         cast_w1(1, 1, 0, 128, "V", "wbf0_1")
         quant_w1(1, 1, "words0", 4096)
         mm1(1, 1, 0)
-        cast_half(1, 2, 0, "V", "wbf0_2")
+        cast_half(1, 2, 0, "V")
+        spot["top"] = spot["top"] + 2048
         cast_half(1, 2, 1, "V")
         quant_half(1, 2, 0, "words0", 6144)
         quant_half(1, 2, 1)
         mm1(1, 2, 0)
         mm1_banks(1, 1, (2, 1), 0, 1)
-        hint01 = place("hint01", [P, PACK * TOK], BF16, "wbf1_2")
+        hint01 = place("hint01", [P, PACK * TOK], BF16, "wbf1_2_0")
         weave_part(0, 1, hint01, 0, TOK, 0, "G")
         gather_g(0, 0, S, "raw0_0", 0)
         quant_part(0, 0, hint00, 0, TOK, "gwin0")
         quant_part(0, 1, hint01, 0, TOK, "gwin0", 2048)
         evac_h(1, 0)
-        hint10 = place("hint10", [P, PACK * TOK], BF16, "wbf1_2")
+        hint10 = place("hint10", [P, PACK * TOK], BF16, "hint00")
         weave_part(1, 0, hint10, 0, TOK, 0, "G")
         mm2(0, 0)
         evac_h(1, 1)

@@ -269,8 +269,8 @@ def tile_list_flow_anomaly_residuals_kernel(tc, tab_words, tab_scales, offs, w1,
         load_g(1)
         load_w4_codes()
         load_w4_scales(nc.sync)
-        load_weight(nc.sync)
         load_g(2)
+        load_weight(nc.sync)
         load_g(3)
         gather_words(0, 0, S)
         gather_words(1, 0, S)
@@ -323,19 +323,19 @@ def tile_list_flow_anomaly_residuals_kernel(tc, tab_words, tab_scales, offs, w1,
         quant_part(1, 0, hint10, 0, TOK, "gwin1")
         hint11 = place("hint11", [P, PACK * TOK], BF16)
         weave_part(1, 1, hint11, 0, TOK, 0, "S")
-        mm2(1, 0)
+        mm2(1, 0, (0, 2, 1, 3))
         quant_part(1, 1, hint11, 0, TOK, "gwin1", 2048)
         mm2(1, 1)
         copy_y(2, 0, "raw1_2", 0)
-        copy_y(3, 0, "raw1_2", 2048)
         finish(0, 0, 0, TOK, "raw1_0", 0)
         finish(1, 0, 0, TOK, "raw1_0", 2048)
         copy_y(2, 1, "diff0_0")
-        copy_y(3, 1, "diff1_0")
+        copy_y(3, 0, "diff1_0")
         finish_fused(2, 0, 0, TOK, "raw0_2", 0)
         finish(0, 1, 0, TOK, "raw1_0", 4096)
-        finish_fused(3, 0, 0, TOK, "raw0_2", 2048)
         finish(1, 1, 0, TOK, "raw1_0", 6144)
+        copy_y(3, 1, "diff0_1")
         finish_fused(2, 1, 0, TOK, "raw0_2", 4096)
+        finish_fused(3, 0, 0, TOK, "raw0_2", 2048)
         finish_fused(3, 1, 0, 384, "raw0_2", 6144)
         finish_fused(3, 1, 384, TOK)

@@ -279,8 +279,8 @@ def tile_list_flow_anomaly_residuals_kernel(tc, tab_words, tab_scales, offs, w1,
         quant_w1(0, 0)
         mm1(0, 0, 0)
         mm1(0, 0, 1, 0, 1)
-        cast_w1(0, 1, 0, 64, "S")
-        cast_w1(0, 1, 64, 128, "V")
+        cast_w1(0, 1, 0, 48, "S")
+        cast_w1(0, 1, 48, 128, "V")
         quant_w1(0, 1)
         mm1(0, 1, 0)
         gather_words(2, 0, S)
@@ -294,12 +294,16 @@ def tile_list_flow_anomaly_residuals_kernel(tc, tab_words, tab_scales, offs, w1,
         evac_h(0, 1)
         hint00 = place("hint00", [P, PACK * TOK], BF16)
         weave_part(0, 0, hint00, 0, TOK, 0, "S")
-        cast_w1(1, 0, 0, 128, "V", "wbf0_0")
-        quant_w1(1, 0, "words0", 2048)
+        cast_half(1, 0, 0, "V")
+        cast_half(1, 0, 1, "V")
+        quant_half(1, 0, 0, "words0", 2048)
+        quant_half(1, 0, 1)
         mm1(1, 0, 0)
         mm1(1, 0, 1, 0, 1)
-        cast_w1(1, 1, 0, 128, "V", "wbf0_1")
-        quant_w1(1, 1, "words0", 4096)
+        cast_half(1, 1, 0, "V")
+        cast_half(1, 1, 1, "V")
+        quant_half(1, 1, 0, "words0", 4096)
+        quant_half(1, 1, 1)
         mm1(1, 1, 0)
         cast_half(1, 2, 0, "V")
         spot["top"] = spot["top"] + 2048

@@ -127,8 +127,11 @@ def tile_list_flow_anomaly_residuals_kernel(tc, tab_words, tab_scales, offs, w1,
                     stop=(a == last),
                 )
 
-        def evac_h(b, s, on_vector=()):
-            for t in range(PACK):
+        def evac_cols(b, s, t, j0, j1):
+            nc.scalar.activation(out=hrow[b][s][:, t, j0:j1], in_=banks[s][t][:, j0:j1], func=ACT.Relu, bias=bias[:, b, t : t + 1])
+
+        def evac_h(b, s, on_vector=(), count=PACK):
+            for t in range(count):
                 if t in on_vector:
                     nc.vector.tensor_scalar(
                         out=hrow[b][s][:, t, :], in0=banks[s][t][:], scalar1=bias[:, b, t : t + 1], scalar2=0.0, op0=ALU.add, op1=ALU.max
@@ -315,20 +318,23 @@ def tile_list_flow_anomaly_residuals_kernel(tc, tab_words, tab_scales, offs, w1,
         hint01 = place("hint01", [P, PACK * TOK], BF16, "wbf1_2_0")
         weave_part(0, 1, hint01, 0, TOK, 0, "G")
         gather_g(0, 0, S, "raw0_0", 0)
-        quant_part(0, 0, hint00, 0, TOK, "gwin0")
-        quant_part(0, 1, hint01, 0, TOK, "gwin0", 2048)
+        quant_part(0, 0, hint00, 0, TOK, "hrow0_1")
+        quant_part(0, 1, hint01, 0, TOK)
         evac_h(1, 0)
         hint10 = place("hint10", [P, PACK * TOK], BF16, "hint00")
         weave_part(1, 0, hint10, 0, TOK, 0, "G")
         mm2(0, 0)
-        evac_h(1, 1)
+        evac_h(1, 1, count=3)
+        evac_cols(1, 1, 3, 0, 256)
+        evac_cols(1, 1, 3, 256, TOK)
         mm2(0, 1)
         gather_g(1, 0, S, "raw0_0", 4096)
-        quant_part(1, 0, hint10, 0, TOK, "gwin1")
+        quant_part(1, 0, hint10, 0, TOK)
         hint11 = place("hint11", [P, PACK * TOK], BF16)
-        weave_part(1, 1, hint11, 0, TOK, 0, "S")
+        weave_part(1, 1, hint11, 0, 256, 0, "S")
+        weave_part(1, 1, hint11, 256, TOK, 256, "S")
         mm2(1, 0, (0, 2, 1, 3))
-        quant_part(1, 1, hint11, 0, TOK, "gwin1", 2048)
+        quant_part(1, 1, hint11, 0, TOK)
         mm2(1, 1)
         copy_y(2, 0, "raw1_2", 0)
         finish(0, 0, 0, TOK, "raw1_0", 0)
@@ -341,5 +347,5 @@ def tile_list_flow_anomaly_residuals_kernel(tc, tab_words, tab_scales, offs, w1,
         copy_y(3, 1, "diff0_1")
         finish_fused(2, 1, 0, TOK, "raw0_2", 4096)
         finish_fused(3, 0, 0, TOK, "raw0_2", 2048)
-        finish_fused(3, 1, 0, 384, "raw0_2", 6144)
-        finish_fused(3, 1, 384, TOK)
+        finish_fused(3, 1, 0, 320, "raw0_2", 6144)
+        finish_fused(3, 1, 320, TOK)

@@ -182,7 +182,7 @@ def tile_list_flow_anomaly_residuals_kernel(tc, tab_words, tab_scales, offs, w1,
             dst = tile[:, PACK * at : PACK * (at + j1 - j0)]
             if eng == "G":
                 nc.gpsimd.tensor_scalar(
-                    out=dst.rearrange("p (j t) -> p j t", t=PACK), in0=src.rearrange("p t j -> p j t"), scalar1=1.0, scalar2=0.0, op0=ALU.mult, op1=ALU.add
+                    out=dst.rearrange("p (c i t) -> p c t i", i=4, t=PACK), in0=src.rearrange("p t (c i) -> p c t i", i=4), scalar1=1.0, scalar2=0.0, op0=ALU.mult, op1=ALU.add
                 )
             else:
                 nc.scalar.copy(out=dst.rearrange("p (c i t) -> p c t i", i=4, t=PACK), in_=src.rearrange("p t (c i) -> p c t i", i=4))

@@ -42,10 +42,10 @@ def tile_list_flow_anomaly_residuals_kernel(tc, tab_words, tab_scales, offs, w1,
                 size = size * n
             if over is None:
                 spot[name] = spot["top"]
-                spot["top"] = spot["top"] + (size + 63) // 64 * 64
+                spot["top"] = spot["top"] + (size + 255) // 256 * 256
             else:
                 spot[name] = spot[over] + at
-            return keep.tile(shape, dtype, name=name, align_bytes=64, offset=spot[name])
+            return keep.tile(shape, dtype, name=name, align_bytes=256, offset=spot[name])
 
         offsets = lists.tile([P, S // 16], U16, name="offsets")
         words = [place(f"words{a}", [P, T], I32) for a in range(KA)]

@@ -25,6 +25,7 @@ NC = N // P
 TOK = 512
 SH = S // TOK
 WIDTH = {F32: 4, I32: 4, U32: 4, BF16: 2, U8: 1}
+KIB = 1024
 
 
 def tile_list_flow_anomaly_residuals_kernel(tc, tab_words, tab_scales, offs, w1, b1, w4_words, w4_scales, gT, wgt, out):
@@ -36,316 +37,293 @@ def tile_list_flow_anomaly_residuals_kernel(tc, tab_words, tab_scales, offs, w1,
 
         spot = {"top": 0}
 
-        def place(name, shape, dtype, over=None, at=0):
+        def place(name, shape, dtype, over=None, at=0, room=0):
             size = WIDTH[dtype]
             for n in shape[1:]:
                 size = size * n
             if over is None:
                 spot[name] = spot["top"]
-                spot["top"] = spot["top"] + (size + 255) // 256 * 256
+                spot["top"] = spot["top"] + (max(size, room) + 255) // 256 * 256
             else:
                 spot[name] = spot[over] + at
             return keep.tile(shape, dtype, name=name, align_bytes=256, offset=spot[name])
 
         offsets = lists.tile([P, S // 16], U16, name="offsets")
-        words = [place(f"words{a}", [P, T], I32) for a in range(KA)]
-        tscale = place("tscale", [P, T // 4], I32)
-        vscale = place("vscale", [P, S], U8)
-        raw = [[place(f"raw{b}_{a}", [P, PACK, KP], F32) for a in range(KA)] for b in range(HB)]
-        wscale = [[place(f"wscale{b}_{a}", [P, KP], U8) for a in range(KA)] for b in range(HB)]
-        bias = place("bias", [P, HB, PACK], F32)
-        weight = place("weight", [P, NC], F32)
-        w4c = place("w4c", [P, HB, 2 * N], U8)
-        w4s = place("w4s", [P, HB, N // 4], I32)
-        gwin = [place(f"gwin{c}", [P, T], F32) for c in range(NC)]
-        hscale = [place(f"hscale{b}", [P, S], U8) for b in range(HB)]
-        hrow = [[place(f"hrow{b}_{s}", [P, PACK, TOK], BF16) for s in range(SH)] for b in range(HB)]
-        hint = {}
-        vcodes, wbf, wcodes, hcodes, gpick, diff, ysb = {}, {}, {}, {}, {}, {}, {}
         banks = [[psum.tile([P, TOK], F32, name=f"bank{s}_{t}") for t in range(PACK)] for s in range(SH)]
+        words, raw, gwin, small = {}, {}, {}, {}
+        vcodes, wbf, wcodes, wscale, hrow, hscale, hcodes, gpick, diff, ysb = {}, {}, {}, {}, {}, {}, {}, {}, {}, {}
 
         def offs_of(j0, j1):
             return offsets[:, j0 // 16 : j1 // 16]
 
-        def load_w1(b, a):
+        def load_w1(b, a, over=None, at=0):
+            raw[b, a] = place(f"raw{b}_{a}", [P, PACK, KP], F32, over, at)[:]
             src = w1[a * KP : (a + 1) * KP, b * KP : (b + 1) * KP]
-            nc.sync.dma_start(out=raw[b][a][:], in_=src.rearrange("(p j) c -> p j c", j=PACK))
+            nc.sync.dma_start(out=raw[b, a], in_=src.rearrange("(p j) c -> p j c", j=PACK))
 
-        def load_words(a):
+        def load_words(a, over=None, at=0):
+            words[a] = place(f"words{a}", [P, T], I32, over, at)
             nc.sync.dma_start(out=words[a][:], in_=tab_words[a].rearrange("p t i -> p (t i)").bitcast(I32))
 
-        def load_g(c):
+        def load_g(c, over=None, at=0):
+            gwin[c] = place(f"gwin{c}", [P, T], F32, over, at)
             nc.sync.dma_start(out=gwin[c][:], in_=gT[c * P : (c + 1) * P, :])
 
-        def cast_w1(b, a, m0, m1, eng, over=None, at=0):
-            if (b, a) not in wbf:
-                wbf[b, a] = place(f"wbf{b}_{a}", [P, PACK * KP], BF16, over, at)
-            dst = wbf[b, a][:].rearrange("p (t m j) -> p m j t", t=PACK, j=PACK)[:, m0:m1]
-            src = raw[b][a][:].rearrange("p j (m t) -> p m j t", t=PACK)[:, m0:m1]
-            if eng == "V":
-                nc.vector.tensor_copy(out=dst, in_=src)
-            else:
-                nc.scalar.copy(out=dst, in_=src)
+        def load_bias(over=None, at=0):
+            small["bias"] = place("bias", [P, HB, PACK], F32, over, at)
+            nc.sync.dma_start(out=small["bias"][:], in_=b1.rearrange("(b p t) -> p b t", b=HB, t=PACK))
 
-        def quant_w1(b, a, over=None, at=0):
-            wcodes[b, a] = place(f"wcodes{b}_{a}", [P, KP], U32, over, at)
-            nc.vector.quantize_mx(out=wcodes[b, a][:].bitcast(FP8X4), scales=wscale[b][a][:], in_=wbf[b, a][:])
+        def load_weight(over=None, at=0):
+            small["weight"] = place("weight", [P, NC], F32, over, at)
+            with nc.allow_non_contiguous_dma(reason="one weight a partition"):
+                nc.sync.dma_start(out=small["weight"][:], in_=wgt.rearrange("(c p) -> p c", p=P))
 
-        def cast_half(b, a, u, eng, over=None, at=0):
-            wbf[b, a, u] = place(f"wbf{b}_{a}_{u}", [P, 2 * KP], BF16, over, at)
-            dst = wbf[b, a, u][:].rearrange("p (t m j) -> p m j t", t=2, j=PACK)
-            src = raw[b][a][:].rearrange("p j (m t) -> p m j t", t=PACK)[:, :, :, 2 * u : 2 * u + 2]
-            if eng == "V":
-                nc.vector.tensor_copy(out=dst, in_=src)
-            else:
-                nc.scalar.copy(out=dst, in_=src)
+        def load_w4_codes(over=None, at=0):
+            small["w4c"] = place("w4c", [P, HB, 2 * N], U8, over, at)
+            nc.sync.dma_start(out=small["w4c"][:].bitcast(I32), in_=w4_words.rearrange("a p n -> p a n").bitcast(I32))
 
-        def quant_half(b, a, u, over=None, at=0):
-            if (b, a) not in wcodes:
-                wcodes[b, a] = place(f"wcodes{b}_{a}", [P, KP], U32, over, at)
-            cols = slice(u * KP // 2, (u + 1) * KP // 2)
-            nc.vector.quantize_mx(out=wcodes[b, a][:, cols].bitcast(FP8X4), scales=wscale[b][a][:, cols], in_=wbf[b, a, u][:])
+        def load_w4_scales(over=None, at=0):
+            small["w4s"] = place("w4s", [P, HB, N // 4], I32, over, at)
+            nc.gpsimd.memset(small["w4s"][:], 0)
+            for r in range(4):
+                nc.sync.dma_start(out=small["w4s"][r:P:32, :, :], in_=w4_scales[:, r:16:4, :].rearrange("a q n -> q a n").bitcast(I32))
 
-        def gather_words(a, j0, j1, over=None, at=0):
-            if a not in vcodes:
-                vcodes[a] = place(f"vcodes{a}", [P, S], I32, over, at)
-            nc.vector.tensor_copy(vcodes[a][:, j0:j1].bitcast(U32), words[a][:].bitcast(U32).indirect(offs_of(j0, j1)))
-
-        def gather_scales():
-            nc.vector.tensor_copy(vscale[:], tscale[:].bitcast(U8).indirect(offs_of(0, S)))
-
-        def mm1(b, a, s, first=0, last=KA - 1):
-            for t in range(PACK):
-                cols = slice(t * P, (t + 1) * P)
-                nc.tensor.matmul_mx(
-                    out=banks[s][t][:],
-                    lhsT=wcodes[b, a][:, cols].bitcast(FP8X4),
-                    lhsT_scale=wscale[b][a][:, cols],
-                    rhs=vcodes[a][:, s * TOK : (s + 1) * TOK].bitcast(FP8X4),
-                    rhs_scale=vscale[PACK * a : P, s * TOK : (s + 1) * TOK],
-                    start=(a == first),
-                    stop=(a == last),
-                )
-
-        def evac_cols(b, s, t, j0, j1):
-            nc.scalar.activation(out=hrow[b][s][:, t, j0:j1], in_=banks[s][t][:, j0:j1], func=ACT.Relu, bias=bias[:, b, t : t + 1])
-
-        def evac_h(b, s, on_vector=(), count=PACK):
-            for t in range(count):
-                if t in on_vector:
-                    nc.vector.tensor_scalar(
-                        out=hrow[b][s][:, t, :], in0=banks[s][t][:], scalar1=bias[:, b, t : t + 1], scalar2=0.0, op0=ALU.add, op1=ALU.max
-                    )
-                else:
-                    nc.scalar.activation(out=hrow[b][s][:, t, :], in_=banks[s][t][:], func=ACT.Relu, bias=bias[:, b, t : t + 1])
-
-        def woven(b, j0, j1, over=None, at=0):
-            tile = place(f"hint{b}_{j0}", [P, PACK * (j1 - j0)], BF16, over, at)
-            for j in range(j0, j1, TOK):
-                hint[b, j // TOK] = tile[:, PACK * (j - j0) : PACK * (j - j0 + TOK)]
-            hint[b, j0, j1] = tile[:]
-
-        def weave_h(b, s, c0, c1, eng):
-            dst = hint[b, s].rearrange("p (c i t) -> p c t i", i=4, t=PACK)[:, c0:c1]
-            src = hrow[b][s][:].rearrange("p t (c i) -> p c t i", i=4)[:, c0:c1]
+        def copy_on(eng, dst, src):
             if eng == "V":
                 nc.vector.tensor_copy(out=dst, in_=src)
             elif eng == "G":
-                dst = hint[b, s].rearrange("p (j t) -> p j t", t=PACK)[:, 4 * c0 : 4 * c1]
-                src = hrow[b][s][:].rearrange("p t j -> p j t")[:, 4 * c0 : 4 * c1]
                 nc.gpsimd.tensor_scalar(out=dst, in0=src, scalar1=1.0, scalar2=0.0, op0=ALU.mult, op1=ALU.add)
             else:
                 nc.scalar.copy(out=dst, in_=src)
 
-        def quant_h(b, j0, j1, over=None, at=0):
-            codes = place(f"hcodes{b}_{j0}", [P, j1 - j0], U32, over, at)
-            nc.vector.quantize_mx(out=codes[:].bitcast(FP8X4), scales=hscale[b][:, j0:j1], in_=hint[b, j0, j1])
-            for j in range(j0, j1, TOK):
-                hcodes[b, j // TOK] = codes[:, j - j0 : j - j0 + TOK]
+        def cast_w1(b, a, m0, m1, eng, room=0):
+            if (b, a) not in wbf:
+                wbf[b, a] = place(f"wbf{b}_{a}", [P, PACK * KP], BF16, room=room)
+            dst = wbf[b, a][:].rearrange("p (t m j) -> p m j t", t=PACK, j=PACK)[:, m0:m1]
+            copy_on(eng, dst, raw[b, a].rearrange("p j (m t) -> p m j t", t=PACK)[:, m0:m1])
+
+        def planes_of(b, a):
+            if (b, a) not in wcodes:
+                wcodes[b, a] = place(f"wcodes{b}_{a}", [P, KP], U32)
+                wscale[b, a] = place(f"wscale{b}_{a}", [P, KP], U8)
+
+        def quant_w1(b, a):
+            planes_of(b, a)
+            nc.vector.quantize_mx(out=wcodes[b, a][:].bitcast(FP8X4), scales=wscale[b, a][:], in_=wbf[b, a][:])
+
+        def cast_half(b, a, u, eng, room=0):
+            wbf[b, a, u] = place(f"wbf{b}_{a}_{u}", [P, 2 * KP], BF16, room=room)
+            dst = wbf[b, a, u][:].rearrange("p (t m j) -> p m j t", t=2, j=PACK)
+            copy_on(eng, dst, raw[b, a].rearrange("p j (m t) -> p m j t", t=PACK)[:, :, :, 2 * u : 2 * u + 2])
+
+        def quant_half(b, a, u):
+            planes_of(b, a)
+            cols = slice(u * KP // 2, (u + 1) * KP // 2)
+            nc.vector.quantize_mx(out=wcodes[b, a][:, cols].bitcast(FP8X4), scales=wscale[b, a][:, cols], in_=wbf[b, a, u][:])
+
+        def gather_words(a):
+            vcodes[a] = place(f"vcodes{a}", [P, S], I32)
+            nc.vector.tensor_copy(vcodes[a][:].bitcast(U32), words[a][:].bitcast(U32).indirect(offs_of(0, S)))
+
+        def mm1_pass(b, a, s, t, first, last):
+            cols = slice(t * P, (t + 1) * P)
+            nc.tensor.matmul_mx(
+                out=banks[s][t][:],
+                lhsT=wcodes[b, a][:, cols].bitcast(FP8X4),
+                lhsT_scale=wscale[b, a][:, cols],
+                rhs=vcodes[a][:, s * TOK : (s + 1) * TOK].bitcast(FP8X4),
+                rhs_scale=small["vscale", a][:].bitcast(U8)[PACK * a : P, s * TOK : (s + 1) * TOK],
+                start=(a == first),
+                stop=(a == last),
+            )
+
+        def mm1(b, a, s, first=0, last=KA - 1):
+            for t in range(PACK):
+                mm1_pass(b, a, s, t, first, last)
 
         def mm1_banks(b, s, passes, first, last):
             for t in range(PACK):
-                cols = slice(t * P, (t + 1) * P)
                 for a in passes:
-                    nc.tensor.matmul_mx(
-                        out=banks[s][t][:],
-                        lhsT=wcodes[b, a][:, cols].bitcast(FP8X4),
-                        lhsT_scale=wscale[b][a][:, cols],
-                        rhs=vcodes[a][:, s * TOK : (s + 1) * TOK].bitcast(FP8X4),
-                        rhs_scale=vscale[PACK * a : P, s * TOK : (s + 1) * TOK],
-                        start=(a == first),
-                        stop=(a == last),
-                    )
+                    mm1_pass(b, a, s, t, first, last)
 
-        def weave_part(b, s, tile, j0, j1, at, eng):
-            src = hrow[b][s][:, :, j0:j1]
-            dst = tile[:, PACK * at : PACK * (at + j1 - j0)]
+        def evac_cols(b, s, t, j0, j1):
+            if (b, s) not in hrow:
+                hrow[b, s] = place(f"hrow{b}_{s}", [P, PACK, TOK], BF16)
+            nc.scalar.activation(out=hrow[b, s][:, t, j0:j1], in_=banks[s][t][:, j0:j1], func=ACT.Relu, bias=small["bias"][:, b, t : t + 1])
+
+        def evac_h(b, s, count=PACK):
+            for t in range(count):
+                evac_cols(b, s, t, 0, TOK)
+
+        def weave(b, s, tile, j0, j1, eng):
+            src = hrow[b, s][:, :, j0:j1]
+            dst = tile[:, PACK * j0 : PACK * j1]
             if eng == "G":
-                nc.gpsimd.tensor_scalar(
-                    out=dst.rearrange("p (c i t) -> p c t i", i=4, t=PACK), in0=src.rearrange("p t (c i) -> p c t i", i=4), scalar1=1.0, scalar2=0.0, op0=ALU.mult, op1=ALU.add
-                )
+                copy_on(eng, dst.rearrange("p (j t) -> p j t", t=PACK), src.rearrange("p t j -> p j t"))
             else:
-                nc.scalar.copy(out=dst.rearrange("p (c i t) -> p c t i", i=4, t=PACK), in_=src.rearrange("p t (c i) -> p c t i", i=4))
+                copy_on(eng, dst.rearrange("p (c i t) -> p c t i", i=4, t=PACK), src.rearrange("p t (c i) -> p c t i", i=4))
 
-        def quant_part(b, s, tile, j0, j1, over=None, at=0):
-            if (b, s) not in hcodes:
-                hcodes[b, s] = place(f"hcodes{b}_{s}", [P, TOK], U32, over, at)[:]
-            nc.vector.quantize_mx(out=hcodes[b, s][:, j0:j1].bitcast(FP8X4), scales=hscale[b][:, s * TOK + j0 : s * TOK + j1], in_=tile[:])
+        def quant_h(b, s, tile, over=None):
+            if b not in hscale:
+                hscale[b] = place(f"hscale{b}", [P, S], U8)
+            hcodes[b, s] = place(f"hcodes{b}_{s}", [P, TOK], U32, over)
+            nc.vector.quantize_mx(out=hcodes[b, s][:].bitcast(FP8X4), scales=hscale[b][:, s * TOK : (s + 1) * TOK], in_=tile[:])
 
         def mm2(b, s, order=(0, 1, 2, 3)):
             for c in order:
                 nc.tensor.matmul_mx(
                     out=banks[s][c][:],
-                    lhsT=w4c[:, b, 2 * c * P : 2 * (c + 1) * P].bitcast(FP4X4),
-                    lhsT_scale=w4s[:, b, :].bitcast(U8)[:, c * P : (c + 1) * P],
-                    rhs=hcodes[b, s].bitcast(FP8X4),
+                    lhsT=small["w4c"][:, b, 2 * c * P : 2 * (c + 1) * P].bitcast(FP4X4),
+                    lhsT_scale=small["w4s"][:, b, :].bitcast(U8)[:, c * P : (c + 1) * P],
+                    rhs=hcodes[b, s][:].bitcast(FP8X4),
                     rhs_scale=hscale[b][:, s * TOK : (s + 1) * TOK],
                     start=(b == 0),
                     stop=(b == HB - 1),
                 )
 
-        def gather_g(c, j0, j1, over=None, at=0):
-            picked = place(f"gpick{c}_{j0}", [P, j1 - j0], F32, over, at)
-            nc.vector.tensor_copy(picked[:], gwin[c][:].indirect(offs_of(j0, j1)))
-            for j in range(j0, j1, TOK):
-                gpick[c, j // TOK] = picked[:, j - j0 : j - j0 + TOK]
+        def gather_g(c):
+            gpick[c] = place(f"gpick{c}", [P, S], F32)
+            nc.vector.tensor_copy(gpick[c][:], gwin[c][:].indirect(offs_of(0, S)))
 
-        def finish(c, s, j0, j1, over=None, at=0):
-            if (c, s) not in diff:
-                diff[c, s] = place(f"diff{c}_{s}", [P, TOK], F32, over, at)
-            d = diff[c, s][:, j0:j1]
-            nc.vector.tensor_tensor(out=d, in0=banks[s][c][:, j0:j1], in1=gpick[c, s][:, j0:j1], op=ALU.subtract)
-            res = place(f"res{c}_{s}", [P, j1 - j0], F32)
-            nc.scalar.activation(out=res[:], in_=d, func=ACT.Abs, scale=weight[:, c : c + 1])
-            nc.sync.dma_start(out=out[c * P : (c + 1) * P, s * TOK + j0 : s * TOK + j1], in_=res[:])
+        def finish(c, s):
+            diff[c, s] = place(f"diff{c}_{s}", [P, TOK], F32)
+            nc.vector.tensor_tensor(out=diff[c, s][:], in0=banks[s][c][:], in1=gpick[c][:, s * TOK : (s + 1) * TOK], op=ALU.subtract)
+            res = place(f"res{c}_{s}", [P, TOK], F32)
+            nc.scalar.activation(out=res[:], in_=diff[c, s][:], func=ACT.Abs, scale=small["weight"][:, c : c + 1])
+            nc.sync.dma_start(out=out[c * P : (c + 1) * P, s * TOK : (s + 1) * TOK], in_=res[:])
 
-        def copy_y(c, s, over=None, at=0):
-            ysb[c, s] = place(f"y{c}_{s}", [P, TOK], F32, over, at)
+        def copy_y(c, s, over=None):
+            ysb[c, s] = place(f"y{c}_{s}", [P, TOK], F32, over)
             nc.scalar.copy(out=ysb[c, s][:], in_=banks[s][c][:])
 
-        def finish_fused(c, s, j0, j1, over=None, at=0):
+        def finish_fused(c, s, j0, j1):
             if (c, s) not in diff:
-                diff[c, s] = place(f"diff{c}_{s}", [P, TOK], F32, over, at)
+                diff[c, s] = place(f"diff{c}_{s}", [P, TOK], F32)
             d = diff[c, s][:, j0:j1]
             nc.vector.tensor_tensor(out=d, in0=gwin[c][:].indirect(offs_of(s * TOK + j0, s * TOK + j1)), in1=ysb[c, s][:, j0:j1], op=ALU.subtract)
-            nc.scalar.activation(out=d, in_=d, func=ACT.Abs, scale=weight[:, c : c + 1])
+            nc.scalar.activation(out=d, in_=d, func=ACT.Abs, scale=small["weight"][:, c : c + 1])
             nc.sync.dma_start(out=out[c * P : (c + 1) * P, s * TOK + j0 : s * TOK + j1], in_=d)
 
-        def load_bias(queue):
-            queue.dma_start(out=bias[:], in_=b1.rearrange("(b p t) -> p b t", b=HB, t=PACK))
+        def stage_scales(over, at):
+            small["tscale"] = place("tscale", [P, T // 4], I32, over, at)
+            for a in range(KA):
+                nc.sync.dma_start(out=small["tscale"][48 + a : 96 : 3, :], in_=tab_scales[a].bitcast(I32))
+            nc.vector.memset(small["tscale"][0:48, :], 0)
+            nc.vector.memset(small["tscale"][96:P, :], 0)
 
-        def load_weight(queue):
-            with nc.allow_non_contiguous_dma(reason="one weight a partition"):
-                queue.dma_start(out=weight[:], in_=wgt.rearrange("(c p) -> p c", p=P))
+        def gather_scales():
+            small["picked"] = place("picked", [P, S // 4], I32)
+            nc.vector.tensor_copy(small["picked"][:].bitcast(U8), small["tscale"][:].bitcast(U8).indirect(offs_of(0, S)))
 
-        def load_w4_codes():
-            nc.sync.dma_start(out=w4c[:].bitcast(I32), in_=w4_words.rearrange("a p n -> p a n").bitcast(I32))
+        def clear_scales():
+            for a in range(KA):
+                small["vscale", a] = place(f"vscale{a}", [P, S // 4], I32)
+                nc.gpsimd.memset(small["vscale", a][:], 0)
 
-        def load_w4_scales(queue):
-            for r in range(4):
-                queue.dma_start(out=w4s[r:P:32, :, :], in_=w4_scales[:, r:16:4, :].rearrange("a q n -> q a n").bitcast(I32))
+        def move_scales(first, last):
+            for a, r in [divmod(i, 4) for i in range(first, last)]:
+                nc.sync.dma_start(out=small["vscale", a][4 * a + r : P : 32, :], in_=small["picked"][48 + 3 * r + a : 96 : 12, :])
 
-        def load_tscale_quadrants(queue):
-            for q in range(4):
-                queue.dma_start(out=tscale[32 * q : 32 * q + 4 * KA, :], in_=tab_scales[:, 4 * q : 4 * q + 4, :].bitcast(I32))
+        def strip(name, size):
+            spot[name] = spot["top"]
+            spot["top"] = spot["top"] + size * KIB
 
-        def load_tscale(first, last):
-            for r, a in [divmod(i, KA) for i in range(first, last)]:
-                nc.sync.dma_start(out=tscale[4 * a + r : P : 32, :], in_=tab_scales[a, r:16:4, :].bitcast(I32))
-
+        for name in ("a", "b", "c", "d"):
+            strip(name, 16)
         nc.sync.dma_start(offsets[:], offs)
-        nc.gpsimd.memset(tscale[:], 0)
-        nc.gpsimd.memset(w4s[:], 0)
-        load_words(0)
-        load_tscale(0, 6)
-        load_words(1)
-        load_tscale(6, 12)
-        load_w1(0, 0)
-        load_w1(0, 1)
-        load_words(2)
-        load_w1(0, 2)
-        load_bias(nc.sync)
-        load_w1(1, 0)
-        load_w1(1, 1)
-        load_w1(1, 2)
-        load_g(0)
-        load_g(1)
-        load_w4_codes()
-        load_w4_scales(nc.sync)
-        load_g(2)
-        load_weight(nc.sync)
-        load_g(3)
-        gather_words(0, 0, S)
-        gather_words(1, 0, S)
+        stage_scales("c", 7 * KIB)
+        load_words(0, "a", 4 * KIB)
+        load_w1(0, 0, "b", 4 * KIB)
+        load_words(1, "d", 4 * KIB)
+        clear_scales()
         gather_scales()
-        cast_w1(0, 0, 0, 128, "S")
+        move_scales(0, 5)
+        load_w1(0, 1, "c")
+        move_scales(5, 7)
+        gather_words(0)
+        load_words(2, "a")
+        move_scales(7, 12)
+        load_w1(0, 2, "a", 8 * KIB)
+        load_bias("c", 8 * KIB)
+        cast_w1(0, 0, 0, 128, "V", room=8 * KIB)
+        load_w1(1, 0, "b")
+        load_w1(1, 1, "b", 8 * KIB)
         quant_w1(0, 0)
+        load_w1(1, 2, "wbf0_0")
         mm1(0, 0, 0)
         mm1(0, 0, 1, 0, 1)
+        gather_words(1)
+        load_g(0, "d")
+        load_g(1, "d", 8 * KIB)
         cast_w1(0, 1, 0, 48, "S")
         cast_w1(0, 1, 48, 128, "V")
         quant_w1(0, 1)
+        load_w4_codes("wbf0_1", KIB)
+        load_w4_scales("wbf0_1")
         mm1(0, 1, 0)
-        gather_words(2, 0, S)
+        gather_words(2)
+        load_g(2, "a")
         cast_half(0, 2, 0, "V")
         cast_half(0, 2, 1, "S")
-        quant_half(0, 2, 0, "words0", 0)
+        quant_half(0, 2, 0)
+        load_weight("wbf0_2_0")
         quant_half(0, 2, 1)
         mm1(0, 2, 0)
         mm1_banks(0, 1, (2, 1), 0, 1)
         evac_h(0, 0)
         evac_h(0, 1)
         hint00 = place("hint00", [P, PACK * TOK], BF16)
-        weave_part(0, 0, hint00, 0, TOK, 0, "S")
+        weave(0, 0, hint00, 0, TOK, "S")
         cast_half(1, 0, 0, "V")
         cast_half(1, 0, 1, "V")
-        quant_half(1, 0, 0, "words0", 2048)
+        load_g(3, "b")
+        quant_half(1, 0, 0)
         quant_half(1, 0, 1)
         mm1(1, 0, 0)
         mm1(1, 0, 1, 0, 1)
         cast_half(1, 1, 0, "V")
         cast_half(1, 1, 1, "V")
-        quant_half(1, 1, 0, "words0", 4096)
+        quant_half(1, 1, 0)
         quant_half(1, 1, 1)
         mm1(1, 1, 0)
-        cast_half(1, 2, 0, "V")
-        spot["top"] = spot["top"] + 2048
+        cast_half(1, 2, 0, "V", room=4 * KIB)
         cast_half(1, 2, 1, "V")
-        quant_half(1, 2, 0, "words0", 6144)
+        quant_half(1, 2, 0)
         quant_half(1, 2, 1)
         mm1(1, 2, 0)
         mm1_banks(1, 1, (2, 1), 0, 1)
+
         hint01 = place("hint01", [P, PACK * TOK], BF16, "wbf1_2_0")
-        weave_part(0, 1, hint01, 0, TOK, 0, "G")
-        gather_g(0, 0, S, "raw0_0", 0)
-        quant_part(0, 0, hint00, 0, TOK, "hrow0_1")
-        quant_part(0, 1, hint01, 0, TOK)
+        weave(0, 1, hint01, 0, TOK, "G")
+        gather_g(0)
+        quant_h(0, 0, hint00, "hrow0_1")
+        quant_h(0, 1, hint01)
         evac_h(1, 0)
         hint10 = place("hint10", [P, PACK * TOK], BF16, "hint00")
-        weave_part(1, 0, hint10, 0, TOK, 0, "G")
+        weave(1, 0, hint10, 0, TOK, "G")
         mm2(0, 0)
         evac_h(1, 1, count=3)
         evac_cols(1, 1, 3, 0, 256)
         evac_cols(1, 1, 3, 256, TOK)
         mm2(0, 1)
-        gather_g(1, 0, S, "raw0_0", 4096)
-        quant_part(1, 0, hint10, 0, TOK)
+        gather_g(1)
+        quant_h(1, 0, hint10)
         hint11 = place("hint11", [P, PACK * TOK], BF16)
-        weave_part(1, 1, hint11, 0, 256, 0, "S")
-        weave_part(1, 1, hint11, 256, TOK, 256, "S")
+        weave(1, 1, hint11, 0, 256, "S")
+        weave(1, 1, hint11, 256, TOK, "S")
         mm2(1, 0, (0, 2, 1, 3))
-        quant_part(1, 1, hint11, 0, TOK)
+        quant_h(1, 1, hint11)
         mm2(1, 1)
-        copy_y(2, 0, "raw1_2", 0)
-        finish(0, 0, 0, TOK, "raw1_0", 0)
-        finish(1, 0, 0, TOK, "raw1_0", 2048)
+        copy_y(2, 0)
+        finish(0, 0)
+        finish(1, 0)
         copy_y(2, 1, "diff0_0")
         copy_y(3, 0, "diff1_0")
-        finish_fused(2, 0, 0, TOK, "raw0_2", 0)
-        finish(0, 1, 0, TOK, "raw1_0", 4096)
-        finish(1, 1, 0, TOK, "raw1_0", 6144)
+        finish_fused(2, 0, 0, TOK)
+        finish(0, 1)
+        finish(1, 1)
         copy_y(3, 1, "diff0_1")
-        finish_fused(2, 1, 0, TOK, "raw0_2", 4096)
-        finish_fused(3, 0, 0, TOK, "raw0_2", 2048)
-        finish_fused(3, 1, 0, 320, "raw0_2", 6144)
+        finish_fused(2, 1, 0, TOK)
+        finish_fused(3, 0, 0, TOK)
+        finish_fused(3, 1, 0, 320)
         finish_fused(3, 1, 320, TOK)

@@ -235,23 +235,23 @@ def tile_list_flow_anomaly_residuals_kernel(tc, tab_words, tab_scales, offs, w1,
         load_words(0, "a", 4 * KIB)
         load_w1(0, 0, "b", 4 * KIB)
         load_words(1, "d", 4 * KIB)
+        load_w1(0, 1)
         clear_scales()
         gather_scales()
-        move_scales(0, 5)
-        load_w1(0, 1, "c")
-        move_scales(5, 7)
+        move_scales(0, 4)
+        load_words(2, "c")
+        move_scales(4, 8)
         gather_words(0)
-        load_words(2, "a")
-        move_scales(7, 12)
-        load_w1(0, 2, "a", 8 * KIB)
+        load_w1(0, 2, "a")
+        move_scales(8, 12)
+        load_w1(1, 0, "a", 8 * KIB)
         load_bias("c", 8 * KIB)
-        cast_w1(0, 0, 0, 128, "V", room=8 * KIB)
-        load_w1(1, 0, "b")
-        load_w1(1, 1, "b", 8 * KIB)
+        cast_w1(0, 0, 0, 128, "V")
+        load_w1(1, 1, "b")
+        load_w1(1, 2, "b", 8 * KIB)
         quant_w1(0, 0)
-        load_w1(1, 2, "wbf0_0")
         mm1(0, 0, 0)
-        mm1(0, 0, 1, 0, 1)
+        mm1(0, 0, 1)
         gather_words(1)
         load_g(0, "d")
         load_g(1, "d", 8 * KIB)
@@ -261,22 +261,23 @@ def tile_list_flow_anomaly_residuals_kernel(tc, tab_words, tab_scales, offs, w1,
         load_w4_codes("wbf0_1", KIB)
         load_w4_scales("wbf0_1")
         mm1(0, 1, 0)
+        mm1(0, 1, 1)
         gather_words(2)
-        load_g(2, "a")
+        load_g(2, "c")
         cast_half(0, 2, 0, "V")
         cast_half(0, 2, 1, "S")
         quant_half(0, 2, 0)
         load_weight("wbf0_2_0")
         quant_half(0, 2, 1)
         mm1(0, 2, 0)
-        mm1_banks(0, 1, (2, 1), 0, 1)
+        mm1(0, 2, 1)
         evac_h(0, 0)
         evac_h(0, 1)
         hint00 = place("hint00", [P, PACK * TOK], BF16)
         weave(0, 0, hint00, 0, TOK, "S")
         cast_half(1, 0, 0, "V")
         cast_half(1, 0, 1, "V")
-        load_g(3, "b")
+        load_g(3, "a", 8 * KIB)
         quant_half(1, 0, 0)
         quant_half(1, 0, 1)
         mm1(1, 0, 0)

@@ -121,8 +121,8 @@ def tile_list_flow_anomaly_residuals_kernel(tc, tab_words, tab_scales, offs, w1,
             cols = slice(u * KP // 2, (u + 1) * KP // 2)
             nc.vector.quantize_mx(out=wcodes[b, a][:, cols].bitcast(FP8X4), scales=wscale[b, a][:, cols], in_=wbf[b, a, u][:])
 
-        def gather_words(a):
-            vcodes[a] = place(f"vcodes{a}", [P, S], I32)
+        def gather_words(a, over=None):
+            vcodes[a] = place(f"vcodes{a}", [P, S], I32, over)
             nc.vector.tensor_copy(vcodes[a][:].bitcast(U32), words[a][:].bitcast(U32).indirect(offs_of(0, S)))
 
         def mm1_pass(b, a, s, t, first, last):
@@ -228,6 +228,13 @@ def tile_list_flow_anomaly_residuals_kernel(tc, tab_words, tab_scales, offs, w1,
             spot[name] = spot["top"]
             spot["top"] = spot["top"] + size * KIB
 
+        def evac_on_vector(b, s, t):
+            if (b, s) not in hrow:
+                hrow[b, s] = place(f"hrow{b}_{s}", [P, PACK, TOK], BF16)
+            nc.vector.tensor_scalar(
+                out=hrow[b, s][:, t, :], in0=banks[s][t][:], scalar1=small["bias"][:, b, t : t + 1], scalar2=0.0, op0=ALU.add, op1=ALU.max
+            )
+
         for name in ("a", "b", "c", "d"):
             strip(name, 16)
         nc.sync.dma_start(offsets[:], offs)
@@ -246,13 +253,14 @@ def tile_list_flow_anomaly_residuals_kernel(tc, tab_words, tab_scales, offs, w1,
         move_scales(8, 12)
         load_w1(1, 0, "a", 8 * KIB)
         load_bias("c", 8 * KIB)
-        cast_w1(0, 0, 0, 128, "V")
+        cast_w1(0, 0, 0, 64, "S")
+        cast_w1(0, 0, 64, 128, "V")
         load_w1(1, 1, "b")
         load_w1(1, 2, "b", 8 * KIB)
         quant_w1(0, 0)
         mm1(0, 0, 0)
         mm1(0, 0, 1)
-        gather_words(1)
+        gather_words(1, "wbf0_0")
         load_g(0, "d")
         load_g(1, "d", 8 * KIB)
         cast_w1(0, 1, 0, 48, "S")
@@ -271,7 +279,10 @@ def tile_list_flow_anomaly_residuals_kernel(tc, tab_words, tab_scales, offs, w1,
         quant_half(0, 2, 1)
         mm1(0, 2, 0)
         mm1(0, 2, 1)
-        evac_h(0, 0)
+        evac_cols(0, 0, 0, 0, TOK)
+        evac_on_vector(0, 0, 1)
+        evac_cols(0, 0, 2, 0, TOK)
+        evac_cols(0, 0, 3, 0, TOK)
         evac_h(0, 1)
         hint00 = place("hint00", [P, PACK * TOK], BF16)
         weave(0, 0, hint00, 0, TOK, "S")

@@ -37,13 +37,13 @@ def tile_list_flow_anomaly_residuals_kernel(tc, tab_words, tab_scales, offs, w1,
 
         spot = {"top": 0}
 
-        def place(name, shape, dtype, over=None, at=0, room=0):
+        def place(name, shape, dtype, over=None, at=0, room=0, ahead=0):
             size = WIDTH[dtype]
             for n in shape[1:]:
                 size = size * n
             if over is None:
-                spot[name] = spot["top"]
-                spot["top"] = spot["top"] + (max(size, room) + 255) // 256 * 256
+                spot[name] = spot["top"] + ahead
+                spot["top"] = spot[name] + (max(size, room) + 255) // 256 * 256
             else:
                 spot[name] = spot[over] + at
             return keep.tile(shape, dtype, name=name, align_bytes=256, offset=spot[name])
@@ -235,6 +235,27 @@ def tile_list_flow_anomaly_residuals_kernel(tc, tab_words, tab_scales, offs, w1,
                 out=hrow[b, s][:, t, :], in0=banks[s][t][:], scalar1=small["bias"][:, b, t : t + 1], scalar2=0.0, op0=ALU.add, op1=ALU.max
             )
 
+        def weave_at(b, s, tile, first, j0, j1, eng):
+            src = hrow[b, s][:, :, j0:j1]
+            dst = tile[:, PACK * (j0 - first) : PACK * (j1 - first)]
+            if eng == "G":
+                copy_on(eng, dst.rearrange("p (j t) -> p j t", t=PACK), src.rearrange("p t j -> p j t"))
+            else:
+                copy_on(eng, dst.rearrange("p (c i t) -> p c t i", i=4, t=PACK), src.rearrange("p t (c i) -> p c t i", i=4))
+
+        def quant_cols(b, s, tile, j0, j1, over=None):
+            if b not in hscale:
+                hscale[b] = place(f"hscale{b}", [P, S], U8)
+            if (b, s) not in hcodes:
+                hcodes[b, s] = place(f"hcodes{b}_{s}", [P, TOK], U32, over)
+            nc.vector.quantize_mx(out=hcodes[b, s][:, j0:j1].bitcast(FP8X4), scales=hscale[b][:, s * TOK + j0 : s * TOK + j1], in_=tile[:])
+
+        def cast_half_rows(b, a, u, m0, m1, eng, room=0, ahead=0):
+            if (b, a, u) not in wbf:
+                wbf[b, a, u] = place(f"wbf{b}_{a}_{u}", [P, 2 * KP], BF16, room=room, ahead=ahead)
+            dst = wbf[b, a, u][:].rearrange("p (t m j) -> p m j t", t=2, j=PACK)[:, m0:m1]
+            copy_on(eng, dst, raw[b, a].rearrange("p j (m t) -> p m j t", t=PACK)[:, m0:m1, :, 2 * u : 2 * u + 2])
+
         for name in ("a", "b", "c", "d"):
             strip(name, 16)
         nc.sync.dma_start(offsets[:], offs)
@@ -272,8 +293,10 @@ def tile_list_flow_anomaly_residuals_kernel(tc, tab_words, tab_scales, offs, w1,
         mm1(0, 1, 1)
         gather_words(2)
         load_g(2, "c")
-        cast_half(0, 2, 0, "V")
-        cast_half(0, 2, 1, "S")
+        cast_half_rows(0, 2, 0, 0, 40, "S")
+        cast_half_rows(0, 2, 0, 40, 128, "V")
+        cast_half_rows(0, 2, 1, 0, 40, "V")
+        cast_half_rows(0, 2, 1, 40, 128, "S")
         quant_half(0, 2, 0)
         load_weight("wbf0_2_0")
         quant_half(0, 2, 1)
@@ -285,12 +308,13 @@ def tile_list_flow_anomaly_residuals_kernel(tc, tab_words, tab_scales, offs, w1,
         evac_cols(0, 0, 3, 0, TOK)
         evac_h(0, 1)
         hint00 = place("hint00", [P, PACK * TOK], BF16)
-        weave(0, 0, hint00, 0, TOK, "S")
+        weave(0, 0, hint00, 208, TOK, "S")
         cast_half(1, 0, 0, "V")
         cast_half(1, 0, 1, "V")
         load_g(3, "a", 8 * KIB)
         quant_half(1, 0, 0)
         quant_half(1, 0, 1)
+        weave(0, 0, hint00, 0, 208, "V")
         mm1(1, 0, 0)
         mm1(1, 0, 1, 0, 1)
         cast_half(1, 1, 0, "V")

@@ -309,6 +309,8 @@ def tile_list_flow_anomaly_residuals_kernel(tc, tab_words, tab_scales, offs, w1,
         evac_h(0, 1)
         hint00 = place("hint00", [P, PACK * TOK], BF16)
         weave(0, 0, hint00, 208, TOK, "S")
+        hint01 = place("hint01", [P, PACK * TOK], BF16)
+        weave(0, 1, hint01, 0, 128, "S")
         cast_half(1, 0, 0, "V")
         cast_half(1, 0, 1, "V")
         load_g(3, "a", 8 * KIB)
@@ -322,15 +324,15 @@ def tile_list_flow_anomaly_residuals_kernel(tc, tab_words, tab_scales, offs, w1,
         quant_half(1, 1, 0)
         quant_half(1, 1, 1)
         mm1(1, 1, 0)
-        cast_half(1, 2, 0, "V", room=4 * KIB)
+        wbf[1, 2, 0] = hint01[:, PACK * 128 : PACK * 384]
+        cast_half_rows(1, 2, 0, 0, 128, "V")
         cast_half(1, 2, 1, "V")
         quant_half(1, 2, 0)
         quant_half(1, 2, 1)
         mm1(1, 2, 0)
         mm1_banks(1, 1, (2, 1), 0, 1)
 
-        hint01 = place("hint01", [P, PACK * TOK], BF16, "wbf1_2_0")
-        weave(0, 1, hint01, 0, TOK, "G")
+        weave(0, 1, hint01, 128, TOK, "G")
         gather_g(0)
         quant_h(0, 0, hint00, "hrow0_1")
         quant_h(0, 1, hint01)

@@ -163,10 +163,10 @@ def tile_list_flow_anomaly_residuals_kernel(tc, tab_words, tab_scales, offs, w1,
             else:
                 copy_on(eng, dst.rearrange("p (c i t) -> p c t i", i=4, t=PACK), src.rearrange("p t (c i) -> p c t i", i=4))
 
-        def quant_h(b, s, tile, over=None):
+        def quant_h(b, s, tile, over=None, at=0):
             if b not in hscale:
                 hscale[b] = place(f"hscale{b}", [P, S], U8)
-            hcodes[b, s] = place(f"hcodes{b}_{s}", [P, TOK], U32, over)
+            hcodes[b, s] = place(f"hcodes{b}_{s}", [P, TOK], U32, over, at)
             nc.vector.quantize_mx(out=hcodes[b, s][:].bitcast(FP8X4), scales=hscale[b][:, s * TOK : (s + 1) * TOK], in_=tile[:])
 
         def mm2(b, s, order=(0, 1, 2, 3)):
@@ -182,27 +182,34 @@ def tile_list_flow_anomaly_residuals_kernel(tc, tab_words, tab_scales, offs, w1,
                 )
 
         def gather_g(c):
-            gpick[c] = place(f"gpick{c}", [P, S], F32)
-            nc.vector.tensor_copy(gpick[c][:], gwin[c][:].indirect(offs_of(0, S)))
+            picked = place(f"gpick{c}", [P, S], F32)
+            nc.vector.tensor_copy(picked[:], gwin[c][:].indirect(offs_of(0, S)))
+            for s in range(SH):
+                gpick[c, s] = picked[:, s * TOK : (s + 1) * TOK]
 
-        def finish(c, s):
-            diff[c, s] = place(f"diff{c}_{s}", [P, TOK], F32)
-            nc.vector.tensor_tensor(out=diff[c, s][:], in0=banks[s][c][:], in1=gpick[c][:, s * TOK : (s + 1) * TOK], op=ALU.subtract)
+        def gather_g_half(c, s):
+            gpick[c, s] = place(f"gpick{c}_{s}", [P, TOK], F32)[:]
+            nc.vector.tensor_copy(gpick[c, s], gwin[c][:].indirect(offs_of(s * TOK, (s + 1) * TOK)))
+
+        def finish(c, s, over=None, at=0, room=0, ahead=0):
+            diff[c, s] = place(f"diff{c}_{s}", [P, TOK], F32, over, at, room, ahead)
+            nc.vector.tensor_tensor(out=diff[c, s][:], in0=banks[s][c][:], in1=gpick[c, s], op=ALU.subtract)
             res = place(f"res{c}_{s}", [P, TOK], F32)
             nc.scalar.activation(out=res[:], in_=diff[c, s][:], func=ACT.Abs, scale=small["weight"][:, c : c + 1])
             nc.sync.dma_start(out=out[c * P : (c + 1) * P, s * TOK : (s + 1) * TOK], in_=res[:])
 
-        def copy_y(c, s, over=None):
-            ysb[c, s] = place(f"y{c}_{s}", [P, TOK], F32, over)
+        def copy_y(c, s, over=None, at=0):
+            ysb[c, s] = place(f"y{c}_{s}", [P, TOK], F32, over, at)
             nc.scalar.copy(out=ysb[c, s][:], in_=banks[s][c][:])
 
-        def finish_fused(c, s, j0, j1):
+        def finish_fused(c, s, j0, j1, over=None):
             if (c, s) not in diff:
                 diff[c, s] = place(f"diff{c}_{s}", [P, TOK], F32)
             d = diff[c, s][:, j0:j1]
             nc.vector.tensor_tensor(out=d, in0=gwin[c][:].indirect(offs_of(s * TOK + j0, s * TOK + j1)), in1=ysb[c, s][:, j0:j1], op=ALU.subtract)
-            nc.scalar.activation(out=d, in_=d, func=ACT.Abs, scale=small["weight"][:, c : c + 1])
-            nc.sync.dma_start(out=out[c * P : (c + 1) * P, s * TOK + j0 : s * TOK + j1], in_=d)
+            res = d if over is None else place(f"res{c}_{s}", [P, j1 - j0], F32, over)[:]
+            nc.scalar.activation(out=res, in_=d, func=ACT.Abs, scale=small["weight"][:, c : c + 1])
+            nc.sync.dma_start(out=out[c * P : (c + 1) * P, s * TOK + j0 : s * TOK + j1], in_=res)
 
         def stage_scales(over, at):
             small["tscale"] = place("tscale", [P, T // 4], I32, over, at)
@@ -307,9 +314,13 @@ def tile_list_flow_anomaly_residuals_kernel(tc, tab_words, tab_scales, offs, w1,
         evac_cols(0, 0, 2, 0, TOK)
         evac_cols(0, 0, 3, 0, TOK)
         evac_h(0, 1)
-        hint00 = place("hint00", [P, PACK * TOK], BF16)
+        pair0 = place("pair0", [P, PACK * 768], BF16)
+        hint10 = pair0[:, : PACK * TOK]
+        hint00 = pair0[:, PACK * 256 :]
         weave(0, 0, hint00, 208, TOK, "S")
-        hint01 = place("hint01", [P, PACK * TOK], BF16)
+        pair1 = place("pair1", [P, PACK * 864], BF16)
+        hint11 = pair1[:, : PACK * TOK]
+        hint01 = pair1[:, PACK * 352 :]
         weave(0, 1, hint01, 0, 128, "S")
         cast_half(1, 0, 0, "V")
         cast_half(1, 0, 1, "V")
@@ -334,30 +345,29 @@ def tile_list_flow_anomaly_residuals_kernel(tc, tab_words, tab_scales, offs, w1,
 
         weave(0, 1, hint01, 128, TOK, "G")
         gather_g(0)
-        quant_h(0, 0, hint00, "hrow0_1")
-        quant_h(0, 1, hint01)
+        quant_cols(0, 0, hint00[:, : PACK * 256], 0, 256, "hrow0_1")
+        quant_cols(0, 0, hint00[:, PACK * 256 :], 256, TOK)
         evac_h(1, 0)
-        hint10 = place("hint10", [P, PACK * TOK], BF16, "hint00")
-        weave(1, 0, hint10, 0, TOK, "G")
+        weave(1, 0, hint10, 112, TOK, "G")
+        weave(1, 0, hint10, 0, 112, "S")
         mm2(0, 0)
-        evac_h(1, 1, count=3)
-        evac_cols(1, 1, 3, 0, 256)
-        evac_cols(1, 1, 3, 256, TOK)
-        mm2(0, 1)
         gather_g(1)
+        evac_h(1, 1)
+        weave(1, 1, hint11, 0, 176, "S")
+        weave(1, 1, hint11, 176, 352, "S")
         quant_h(1, 0, hint10)
-        hint11 = place("hint11", [P, PACK * TOK], BF16)
-        weave(1, 1, hint11, 0, 256, "S")
-        weave(1, 1, hint11, 256, TOK, "S")
-        mm2(1, 0, (0, 2, 1, 3))
-        quant_h(1, 1, hint11)
-        mm2(1, 1)
+        quant_h(0, 1, hint01, "hrow1_0")
+        weave(1, 1, hint11, 352, TOK, "G")
+        mm2(1, 0, (0, 1, 2, 3))
+        mm2(0, 1)
         copy_y(2, 0)
         finish(0, 0)
         finish(1, 0)
+        quant_h(1, 1, hint11, "hcodes1_0")
+        mm2(1, 1)
+        copy_y(3, 0)
         copy_y(2, 1, "diff0_0")
-        copy_y(3, 0, "diff1_0")
-        finish_fused(2, 0, 0, TOK)
+        finish_fused(2, 0, 0, TOK, "hcodes1_1")
         finish(0, 1)
         finish(1, 1)
         copy_y(3, 1, "diff0_1")

@@ -318,10 +318,10 @@ def tile_list_flow_anomaly_residuals_kernel(tc, tab_words, tab_scales, offs, w1,
         hint10 = pair0[:, : PACK * TOK]
         hint00 = pair0[:, PACK * 256 :]
         weave(0, 0, hint00, 208, TOK, "S")
-        pair1 = place("pair1", [P, PACK * 864], BF16)
+        pair1 = place("pair1", [P, PACK * 896], BF16)
         hint11 = pair1[:, : PACK * TOK]
-        hint01 = pair1[:, PACK * 352 :]
-        weave(0, 1, hint01, 0, 128, "S")
+        hint01 = pair1[:, PACK * 384 :]
+        weave(0, 1, hint01, 0, 160, "S")
         cast_half(1, 0, 0, "V")
         cast_half(1, 0, 1, "V")
         load_g(3, "a", 8 * KIB)
@@ -335,7 +335,7 @@ def tile_list_flow_anomaly_residuals_kernel(tc, tab_words, tab_scales, offs, w1,
         quant_half(1, 1, 0)
         quant_half(1, 1, 1)
         mm1(1, 1, 0)
-        wbf[1, 2, 0] = hint01[:, PACK * 128 : PACK * 384]
+        wbf[1, 2, 0] = hint01[:, PACK * 160 : PACK * 416]
         cast_half_rows(1, 2, 0, 0, 128, "V")
         cast_half(1, 2, 1, "V")
         quant_half(1, 2, 0)
@@ -343,21 +343,21 @@ def tile_list_flow_anomaly_residuals_kernel(tc, tab_words, tab_scales, offs, w1,
         mm1(1, 2, 0)
         mm1_banks(1, 1, (2, 1), 0, 1)
 
-        weave(0, 1, hint01, 128, TOK, "G")
+        weave(0, 1, hint01, 160, TOK, "G")
         gather_g(0)
         quant_cols(0, 0, hint00[:, : PACK * 256], 0, 256, "hrow0_1")
         quant_cols(0, 0, hint00[:, PACK * 256 :], 256, TOK)
         evac_h(1, 0)
-        weave(1, 0, hint10, 112, TOK, "G")
-        weave(1, 0, hint10, 0, 112, "S")
+        weave(1, 0, hint10, 128, TOK, "G")
+        weave(1, 0, hint10, 0, 128, "S")
         mm2(0, 0)
         gather_g(1)
         evac_h(1, 1)
-        weave(1, 1, hint11, 0, 176, "S")
-        weave(1, 1, hint11, 176, 352, "S")
+        weave(1, 1, hint11, 0, 192, "S")
+        weave(1, 1, hint11, 192, 384, "S")
         quant_h(1, 0, hint10)
         quant_h(0, 1, hint01, "hrow1_0")
-        weave(1, 1, hint11, 352, TOK, "G")
+        weave(1, 1, hint11, 384, TOK, "G")
         mm2(1, 0, (0, 1, 2, 3))
         mm2(0, 1)
         copy_y(2, 0)

from contextlib import ExitStack

import concourse.mybir as mybir

K, H, N, T, S = 1536, 1024, 512, 2048, 1024
FLOPS = 2 * S * (K * H + H * N)

F32 = mybir.dt.float32
BF16 = mybir.dt.bfloat16
I32 = mybir.dt.int32
U32 = mybir.dt.uint32
U16 = mybir.dt.uint16
U8 = mybir.dt.uint8
FP8X4 = mybir.dt.float8_e4m3fn_x4
FP4X4 = mybir.dt.float4_e2m1fn_x4
ACT = mybir.ActivationFunctionType
ALU = mybir.AluOpType

P = 128
PACK = 4
KP = P * PACK
KA = K // KP
HB = H // KP
NC = N // P
TOK = 512
SH = S // TOK
WIDTH = {F32: 4, I32: 4, U32: 4, BF16: 2, U8: 1}
KIB = 1024


def tile_list_flow_anomaly_residuals_kernel(tc, tab_words, tab_scales, offs, w1, b1, w4_words, w4_scales, gT, wgt, out):
    nc = tc.nc
    with ExitStack() as ctx:
        lists = ctx.enter_context(tc.tile_pool(name="lists", bufs=1))
        keep = ctx.enter_context(tc.tile_pool(name="keep", bufs=1))
        psum = ctx.enter_context(tc.psum_pool(name="psum", bufs=1))

        spot = {"top": 0}

        def place(name, shape, dtype, over=None, at=0, room=0, ahead=0):
            size = WIDTH[dtype]
            for n in shape[1:]:
                size = size * n
            if over is None:
                spot[name] = spot["top"] + ahead
                spot["top"] = spot[name] + (max(size, room) + 255) // 256 * 256
            else:
                spot[name] = spot[over] + at
            return keep.tile(shape, dtype, name=name, align_bytes=256, offset=spot[name])

        offsets = lists.tile([P, S // 16], U16, name="offsets")
        banks = [[psum.tile([P, TOK], F32, name=f"bank{s}_{t}") for t in range(PACK)] for s in range(SH)]
        words, raw, gwin, small = {}, {}, {}, {}
        vcodes, wbf, wcodes, wscale, hrow, hscale, hcodes, gpick, diff, ysb = {}, {}, {}, {}, {}, {}, {}, {}, {}, {}

        def offs_of(j0, j1):
            return offsets[:, j0 // 16 : j1 // 16]

        def load_w1(b, a, over=None, at=0):
            raw[b, a] = place(f"raw{b}_{a}", [P, PACK, KP], F32, over, at)[:]
            src = w1[a * KP : (a + 1) * KP, b * KP : (b + 1) * KP]
            nc.sync.dma_start(out=raw[b, a], in_=src.rearrange("(p j) c -> p j c", j=PACK))

        def load_words(a, over=None, at=0):
            words[a] = place(f"words{a}", [P, T], I32, over, at)
            nc.sync.dma_start(out=words[a][:], in_=tab_words[a].rearrange("p t i -> p (t i)").bitcast(I32))

        def load_g(c, over=None, at=0):
            gwin[c] = place(f"gwin{c}", [P, T], F32, over, at)
            nc.sync.dma_start(out=gwin[c][:], in_=gT[c * P : (c + 1) * P, :])

        def load_bias(over=None, at=0):
            small["bias"] = place("bias", [P, HB, PACK], F32, over, at)
            nc.sync.dma_start(out=small["bias"][:], in_=b1.rearrange("(b p t) -> p b t", b=HB, t=PACK))

        def load_weight(over=None, at=0):
            small["weight"] = place("weight", [P, NC], F32, over, at)
            with nc.allow_non_contiguous_dma(reason="one weight a partition"):
                nc.sync.dma_start(out=small["weight"][:], in_=wgt.rearrange("(c p) -> p c", p=P))

        def load_w4_codes(over=None, at=0):
            small["w4c"] = place("w4c", [P, HB, 2 * N], U8, over, at)
            nc.sync.dma_start(out=small["w4c"][:].bitcast(I32), in_=w4_words.rearrange("a p n -> p a n").bitcast(I32))

        def load_w4_scales(over=None, at=0):
            small["w4s"] = place("w4s", [P, HB, N // 4], I32, over, at)
            nc.gpsimd.memset(small["w4s"][:], 0)
            for r in range(4):
                nc.sync.dma_start(out=small["w4s"][r:P:32, :, :], in_=w4_scales[:, r:16:4, :].rearrange("a q n -> q a n").bitcast(I32))

        def copy_on(eng, dst, src):
            if eng == "V":
                nc.vector.tensor_copy(out=dst, in_=src)
            elif eng == "G":
                nc.gpsimd.tensor_scalar(out=dst, in0=src, scalar1=1.0, scalar2=0.0, op0=ALU.mult, op1=ALU.add)
            else:
                nc.scalar.copy(out=dst, in_=src)

        def cast_w1(b, a, m0, m1, eng, room=0):
            if (b, a) not in wbf:
                wbf[b, a] = place(f"wbf{b}_{a}", [P, PACK * KP], BF16, room=room)
            dst = wbf[b, a][:].rearrange("p (t m j) -> p m j t", t=PACK, j=PACK)[:, m0:m1]
            copy_on(eng, dst, raw[b, a].rearrange("p j (m t) -> p m j t", t=PACK)[:, m0:m1])

        def planes_of(b, a):
            if (b, a) not in wcodes:
                wcodes[b, a] = place(f"wcodes{b}_{a}", [P, KP], U32)
                wscale[b, a] = place(f"wscale{b}_{a}", [P, KP], U8)

        def quant_w1(b, a):
            planes_of(b, a)
            nc.vector.quantize_mx(out=wcodes[b, a][:].bitcast(FP8X4), scales=wscale[b, a][:], in_=wbf[b, a][:])

        def cast_half(b, a, u, eng, room=0):
            wbf[b, a, u] = place(f"wbf{b}_{a}_{u}", [P, 2 * KP], BF16, room=room)
            dst = wbf[b, a, u][:].rearrange("p (t m j) -> p m j t", t=2, j=PACK)
            copy_on(eng, dst, raw[b, a].rearrange("p j (m t) -> p m j t", t=PACK)[:, :, :, 2 * u : 2 * u + 2])

        def quant_half(b, a, u):
            planes_of(b, a)
            cols = slice(u * KP // 2, (u + 1) * KP // 2)
            nc.vector.quantize_mx(out=wcodes[b, a][:, cols].bitcast(FP8X4), scales=wscale[b, a][:, cols], in_=wbf[b, a, u][:])

        def gather_words(a, over=None):
            vcodes[a] = place(f"vcodes{a}", [P, S], I32, over)
            nc.vector.tensor_copy(vcodes[a][:].bitcast(U32), words[a][:].bitcast(U32).indirect(offs_of(0, S)))

        def mm1_pass(b, a, s, t, first, last):
            cols = slice(t * P, (t + 1) * P)
            nc.tensor.matmul_mx(
                out=banks[s][t][:],
                lhsT=wcodes[b, a][:, cols].bitcast(FP8X4),
                lhsT_scale=wscale[b, a][:, cols],
                rhs=vcodes[a][:, s * TOK : (s + 1) * TOK].bitcast(FP8X4),
                rhs_scale=small["vscale", a][:].bitcast(U8)[PACK * a : P, s * TOK : (s + 1) * TOK],
                start=(a == first),
                stop=(a == last),
            )

        def mm1(b, a, s, first=0, last=KA - 1):
            for t in range(PACK):
                mm1_pass(b, a, s, t, first, last)

        def mm1_banks(b, s, passes, first, last):
            for t in range(PACK):
                for a in passes:
                    mm1_pass(b, a, s, t, first, last)

        def evac_cols(b, s, t, j0, j1):
            if (b, s) not in hrow:
                hrow[b, s] = place(f"hrow{b}_{s}", [P, PACK, TOK], BF16)
            nc.scalar.activation(out=hrow[b, s][:, t, j0:j1], in_=banks[s][t][:, j0:j1], func=ACT.Relu, bias=small["bias"][:, b, t : t + 1])

        def evac_h(b, s, count=PACK):
            for t in range(count):
                evac_cols(b, s, t, 0, TOK)

        def weave(b, s, tile, j0, j1, eng):
            src = hrow[b, s][:, :, j0:j1]
            dst = tile[:, PACK * j0 : PACK * j1]
            if eng == "G":
                copy_on(eng, dst.rearrange("p (j t) -> p j t", t=PACK), src.rearrange("p t j -> p j t"))
            else:
                copy_on(eng, dst.rearrange("p (c i t) -> p c t i", i=4, t=PACK), src.rearrange("p t (c i) -> p c t i", i=4))

        def quant_h(b, s, tile, over=None, at=0):
            if b not in hscale:
                hscale[b] = place(f"hscale{b}", [P, S], U8)
            hcodes[b, s] = place(f"hcodes{b}_{s}", [P, TOK], U32, over, at)
            nc.vector.quantize_mx(out=hcodes[b, s][:].bitcast(FP8X4), scales=hscale[b][:, s * TOK : (s + 1) * TOK], in_=tile[:])

        def mm2(b, s, order=(0, 1, 2, 3)):
            for c in order:
                nc.tensor.matmul_mx(
                    out=banks[s][c][:],
                    lhsT=small["w4c"][:, b, 2 * c * P : 2 * (c + 1) * P].bitcast(FP4X4),
                    lhsT_scale=small["w4s"][:, b, :].bitcast(U8)[:, c * P : (c + 1) * P],
                    rhs=hcodes[b, s][:].bitcast(FP8X4),
                    rhs_scale=hscale[b][:, s * TOK : (s + 1) * TOK],
                    start=(b == 0),
                    stop=(b == HB - 1),
                )

        def gather_g(c):
            picked = place(f"gpick{c}", [P, S], F32)
            nc.vector.tensor_copy(picked[:], gwin[c][:].indirect(offs_of(0, S)))
            for s in range(SH):
                gpick[c, s] = picked[:, s * TOK : (s + 1) * TOK]

        def gather_g_half(c, s):
            gpick[c, s] = place(f"gpick{c}_{s}", [P, TOK], F32)[:]
            nc.vector.tensor_copy(gpick[c, s], gwin[c][:].indirect(offs_of(s * TOK, (s + 1) * TOK)))

        def finish(c, s, over=None, at=0, room=0, ahead=0):
            diff[c, s] = place(f"diff{c}_{s}", [P, TOK], F32, over, at, room, ahead)
            nc.vector.tensor_tensor(out=diff[c, s][:], in0=banks[s][c][:], in1=gpick[c, s], op=ALU.subtract)
            res = place(f"res{c}_{s}", [P, TOK], F32)
            nc.scalar.activation(out=res[:], in_=diff[c, s][:], func=ACT.Abs, scale=small["weight"][:, c : c + 1])
            nc.sync.dma_start(out=out[c * P : (c + 1) * P, s * TOK : (s + 1) * TOK], in_=res[:])

        def copy_y(c, s, over=None, at=0):
            ysb[c, s] = place(f"y{c}_{s}", [P, TOK], F32, over, at)
            nc.scalar.copy(out=ysb[c, s][:], in_=banks[s][c][:])

        def finish_fused(c, s, j0, j1, over=None):
            if (c, s) not in diff:
                diff[c, s] = place(f"diff{c}_{s}", [P, TOK], F32)
            d = diff[c, s][:, j0:j1]
            nc.vector.tensor_tensor(out=d, in0=gwin[c][:].indirect(offs_of(s * TOK + j0, s * TOK + j1)), in1=ysb[c, s][:, j0:j1], op=ALU.subtract)
            res = d if over is None else place(f"res{c}_{s}", [P, j1 - j0], F32, over)[:]
            nc.scalar.activation(out=res, in_=d, func=ACT.Abs, scale=small["weight"][:, c : c + 1])
            nc.sync.dma_start(out=out[c * P : (c + 1) * P, s * TOK + j0 : s * TOK + j1], in_=res)

        def stage_scales(over, at):
            small["tscale"] = place("tscale", [P, T // 4], I32, over, at)
            for a in range(KA):
                nc.sync.dma_start(out=small["tscale"][48 + a : 96 : 3, :], in_=tab_scales[a].bitcast(I32))
            nc.vector.memset(small["tscale"][0:48, :], 0)
            nc.vector.memset(small["tscale"][96:P, :], 0)

        def gather_scales():
            small["picked"] = place("picked", [P, S // 4], I32)
            nc.vector.tensor_copy(small["picked"][:].bitcast(U8), small["tscale"][:].bitcast(U8).indirect(offs_of(0, S)))

        def clear_scales():
            for a in range(KA):
                small["vscale", a] = place(f"vscale{a}", [P, S // 4], I32)
                nc.gpsimd.memset(small["vscale", a][:], 0)

        def move_scales(first, last):
            for a, r in [divmod(i, 4) for i in range(first, last)]:
                nc.sync.dma_start(out=small["vscale", a][4 * a + r : P : 32, :], in_=small["picked"][48 + 3 * r + a : 96 : 12, :])

        def strip(name, size):
            spot[name] = spot["top"]
            spot["top"] = spot["top"] + size * KIB

        def evac_on_vector(b, s, t):
            if (b, s) not in hrow:
                hrow[b, s] = place(f"hrow{b}_{s}", [P, PACK, TOK], BF16)
            nc.vector.tensor_scalar(
                out=hrow[b, s][:, t, :], in0=banks[s][t][:], scalar1=small["bias"][:, b, t : t + 1], scalar2=0.0, op0=ALU.add, op1=ALU.max
            )

        def weave_at(b, s, tile, first, j0, j1, eng):
            src = hrow[b, s][:, :, j0:j1]
            dst = tile[:, PACK * (j0 - first) : PACK * (j1 - first)]
            if eng == "G":
                copy_on(eng, dst.rearrange("p (j t) -> p j t", t=PACK), src.rearrange("p t j -> p j t"))
            else:
                copy_on(eng, dst.rearrange("p (c i t) -> p c t i", i=4, t=PACK), src.rearrange("p t (c i) -> p c t i", i=4))

        def quant_cols(b, s, tile, j0, j1, over=None):
            if b not in hscale:
                hscale[b] = place(f"hscale{b}", [P, S], U8)
            if (b, s) not in hcodes:
                hcodes[b, s] = place(f"hcodes{b}_{s}", [P, TOK], U32, over)
            nc.vector.quantize_mx(out=hcodes[b, s][:, j0:j1].bitcast(FP8X4), scales=hscale[b][:, s * TOK + j0 : s * TOK + j1], in_=tile[:])

        def cast_half_rows(b, a, u, m0, m1, eng, room=0, ahead=0):
            if (b, a, u) not in wbf:
                wbf[b, a, u] = place(f"wbf{b}_{a}_{u}", [P, 2 * KP], BF16, room=room, ahead=ahead)
            dst = wbf[b, a, u][:].rearrange("p (t m j) -> p m j t", t=2, j=PACK)[:, m0:m1]
            copy_on(eng, dst, raw[b, a].rearrange("p j (m t) -> p m j t", t=PACK)[:, m0:m1, :, 2 * u : 2 * u + 2])

        for name in ("a", "b", "c", "d"):
            strip(name, 16)
        nc.sync.dma_start(offsets[:], offs)
        stage_scales("c", 7 * KIB)
        load_words(0, "a", 4 * KIB)
        load_w1(0, 0, "b", 4 * KIB)
        load_words(1, "d", 4 * KIB)
        load_w1(0, 1)
        clear_scales()
        gather_scales()
        move_scales(0, 4)
        load_words(2, "c")
        move_scales(4, 8)
        gather_words(0)
        load_w1(0, 2, "a")
        move_scales(8, 12)
        load_w1(1, 0, "a", 8 * KIB)
        load_bias("c", 8 * KIB)
        cast_w1(0, 0, 0, 64, "S")
        cast_w1(0, 0, 64, 128, "V")
        load_w1(1, 1, "b")
        load_w1(1, 2, "b", 8 * KIB)
        quant_w1(0, 0)
        mm1(0, 0, 0)
        mm1(0, 0, 1)
        gather_words(1, "wbf0_0")
        load_g(0, "d")
        load_g(1, "d", 8 * KIB)
        cast_w1(0, 1, 0, 48, "S")
        cast_w1(0, 1, 48, 128, "V")
        quant_w1(0, 1)
        load_w4_codes("wbf0_1", KIB)
        load_w4_scales("wbf0_1")
        mm1(0, 1, 0)
        mm1(0, 1, 1)
        gather_words(2)
        load_g(2, "c")
        cast_half_rows(0, 2, 0, 0, 40, "S")
        cast_half_rows(0, 2, 0, 40, 128, "V")
        cast_half_rows(0, 2, 1, 0, 40, "V")
        cast_half_rows(0, 2, 1, 40, 128, "S")
        quant_half(0, 2, 0)
        load_weight("wbf0_2_0")
        quant_half(0, 2, 1)
        mm1(0, 2, 0)
        mm1(0, 2, 1)
        evac_cols(0, 0, 0, 0, TOK)
        evac_on_vector(0, 0, 1)
        evac_cols(0, 0, 2, 0, TOK)
        evac_cols(0, 0, 3, 0, TOK)
        evac_h(0, 1)
        pair0 = place("pair0", [P, PACK * 768], BF16)
        hint10 = pair0[:, : PACK * TOK]
        hint00 = pair0[:, PACK * 256 :]
        weave(0, 0, hint00, 208, TOK, "S")
        pair1 = place("pair1", [P, PACK * 896], BF16)
        hint11 = pair1[:, : PACK * TOK]
        hint01 = pair1[:, PACK * 384 :]
        weave(0, 1, hint01, 0, 160, "S")
        cast_half(1, 0, 0, "V")
        cast_half(1, 0, 1, "V")
        load_g(3, "a", 8 * KIB)
        quant_half(1, 0, 0)
        quant_half(1, 0, 1)
        weave(0, 0, hint00, 0, 208, "V")
        mm1(1, 0, 0)
        mm1(1, 0, 1, 0, 1)
        cast_half(1, 1, 0, "V")
        cast_half(1, 1, 1, "V")
        quant_half(1, 1, 0)
        quant_half(1, 1, 1)
        mm1(1, 1, 0)
        wbf[1, 2, 0] = hint01[:, PACK * 160 : PACK * 416]
        cast_half_rows(1, 2, 0, 0, 128, "V")
        cast_half(1, 2, 1, "V")
        quant_half(1, 2, 0)
        quant_half(1, 2, 1)
        mm1(1, 2, 0)
        mm1_banks(1, 1, (2, 1), 0, 1)

        weave(0, 1, hint01, 160, TOK, "G")
        gather_g(0)
        quant_cols(0, 0, hint00[:, : PACK * 256], 0, 256, "hrow0_1")
        quant_cols(0, 0, hint00[:, PACK * 256 :], 256, TOK)
        evac_h(1, 0)
        weave(1, 0, hint10, 128, TOK, "G")
        weave(1, 0, hint10, 0, 128, "S")
        mm2(0, 0)
        gather_g(1)
        evac_h(1, 1)
        weave(1, 1, hint11, 0, 192, "S")
        weave(1, 1, hint11, 192, 384, "S")
        quant_h(1, 0, hint10)
        quant_h(0, 1, hint01, "hrow1_0")
        weave(1, 1, hint11, 384, TOK, "G")
        mm2(1, 0, (0, 1, 2, 3))
        mm2(0, 1)
        copy_y(2, 0)
        finish(0, 0)
        finish(1, 0)
        quant_h(1, 1, hint11, "hcodes1_0")
        mm2(1, 1)
        copy_y(3, 0)
        copy_y(2, 1, "diff0_0")
        finish_fused(2, 0, 0, TOK, "hcodes1_1")
        finish(0, 1)
        finish(1, 1)
        copy_y(3, 1, "diff0_1")
        finish_fused(2, 1, 0, TOK)
        finish_fused(3, 0, 0, TOK)
        finish_fused(3, 1, 0, 320)
        finish_fused(3, 1, 320, TOK)
